import numpy as np
import ml_dtypes


def mxq(x, axis, fmt="e4m3"):
    dtype, down = {"e4m3": (ml_dtypes.float8_e4m3fn, 7), "e5m2": (ml_dtypes.float8_e5m2, 14)}[fmt]
    v = np.moveaxis(np.asarray(x, np.float32).astype(ml_dtypes.bfloat16).astype(np.float64), axis, -1)
    blocks = v.reshape(v.shape[:-1] + (-1, 32))
    amax = np.abs(blocks).max(-1, keepdims=True)
    byte = np.maximum(np.where(amax > 0, np.frexp(amax)[1] - 1 + 127, 0) - down, 1)
    scale = np.exp2(byte - 127.0)
    codes = (blocks / scale).astype(np.float32).astype(dtype).astype(np.float64)
    return np.moveaxis((codes * scale).reshape(v.shape), -1, axis)


WIDE = False


def mx_kscale(k):
    if not WIDE:
        return np.ones(k)
    levels = np.array([10, -10, 5, -5, 0])
    if k % 512:
        return np.exp2(np.random.permutation(np.resize(levels, k // 32))).repeat(32)
    a = np.empty((k // 512, 16))
    for p in range(k // 512):
        a[p, :8] = np.random.permutation(np.resize(levels, 8))
        for g in range(8):
            far = levels[np.abs(levels - a[p, g]) >= 10]
            a[p, g + 8] = far[np.random.randint(len(far))]
    return np.exp2(a.ravel()).repeat(32)


def f64(x):
    return np.asarray(x).astype(np.float64)


def striped(idx):
    return np.tile(idx.reshape(-1, 16).T, (8, 1)).astype(np.uint16)


def unstriped(offs):
    return offs[:16].T.reshape(-1).astype(np.int64)


def pack_weight(w):
    k, n = w.shape
    w = f64(np.asarray(w, np.float32).astype(ml_dtypes.bfloat16)).reshape(k // 32, 32, n)
    amax = np.abs(w).max(1)
    byte = np.clip(np.where(amax > 0, np.frexp(amax)[1] - 1 + 127 - 7, 1), 1, 254)
    scaled = (w * np.exp2(127.0 - byte)[:, None, :]).reshape(k, n).astype(np.float32)
    words = np.ascontiguousarray(scaled.reshape(k // 512, 128, 4, n).transpose(0, 1, 3, 2)).astype(ml_dtypes.float8_e4m3fn).view(np.uint8)
    return words, np.ascontiguousarray(byte.astype(np.uint8).reshape(k // 512, 16, n))


def unpack_weight(words, scales):
    g, p, n, _ = words.shape
    vals = np.ascontiguousarray(words).view(ml_dtypes.float8_e4m3fn).astype(np.float64) * np.repeat(np.exp2(scales.astype(np.float64) - 127.0), 8, axis=1)[..., None]
    return vals.transpose(0, 1, 3, 2).reshape(g * 512, n)


def silu(v):
    return v / (1.0 + np.exp(-np.maximum(v, -700.0)))


K, T, S, N = 512, 2048, 1024, 128
P = 2 ** 7


def setup_inputs():
    n = np.random.standard_normal
    s = mx_kscale(K)[:, None]
    packed_xT = pack_weight(n((K, T)) * s)
    return {
        "x_words": packed_xT[0],
        "x_scales": packed_xT[1],
        "mean": np.tile(0.3 * np.random.standard_normal(T), (P, 1)).astype(np.float32),
        "inv": np.tile(np.random.uniform(0.5, 2.0, T), (P, 1)).astype(np.float32),
        "gsum": n((N, 1)).astype(np.float32),
        "b": (0.3 * n((N, 1))).astype(np.float32),
        "w1": (n((K, N)) / np.sqrt(K) / s).astype(np.float32),
        "offs": striped(np.random.permutation(T)[:S]),
    }


def reference(x_words, x_scales, mean, inv, gsum, b, w1, offs):
    xq = unpack_weight(x_words, x_scales)[:, unstriped(offs)]
    y = mxq(f64(w1), 0, "e4m3").T @ xq
    mg = f64(mean)[:1][:, unstriped(offs)]
    ig = f64(inv)[:1][:, unstriped(offs)]
    return silu((y - (f64(gsum) * mg)) * ig + f64(b))

@@ -1,0 +1,125 @@
+from contextlib import ExitStack
+
+import concourse.mybir as mybir
+from concourse.masks import make_identity
+
+K, T, S, N = 512, 2048, 1024, 128
+P = 128
+FLOPS = 2 * K * N * S
+BYTES = K * T + (K // 32) * T + 2 * 4 * T + 4 * K * N + 2 * 4 * N + 2 * P * (S // 16) + 4 * N * S
+
+F32 = mybir.dt.float32
+BF16 = mybir.dt.bfloat16
+I32 = mybir.dt.int32
+U32 = mybir.dt.uint32
+U16 = mybir.dt.uint16
+U8 = mybir.dt.uint8
+FP8X4 = mybir.dt.float8_e4m3fn_x4
+ACT = mybir.ActivationFunctionType
+ALU = mybir.AluOpType
+
+MEAN_ROW, INV_ROW = 126, 127
+HALF = 512
+STAGE = 256
+BLOCK = 128
+
+
+def tile_picked_lnfold_silu_p_kernel(tc, x_words, x_scales, mean, inv, gsum, b, w1, offs, out):
+    nc = tc.nc
+    with ExitStack() as ctx:
+        keep = ctx.enter_context(tc.tile_pool(name="keep", bufs=1))
+        ring = ctx.enter_context(tc.tile_pool(name="ring", bufs=2))
+        psum = ctx.enter_context(tc.psum_pool(name="psum", bufs=4))
+
+        offsets = keep.tile([P, S // 16], U16, name="offsets")
+        stats = keep.tile([P, T], F32, name="stats")
+        words = keep.tile([P, T], I32, name="words", align_bytes=64)
+        planes = keep.tile([P, T], U8, name="planes", align_bytes=64)
+        w_raw = keep.tile([P, 4, N], F32, name="w_raw")
+        gsum_col = keep.tile([P, 1], F32, name="gsum_col")
+        b_col = keep.tile([P, 1], F32, name="b_col")
+        ident = keep.tile([P, P], F32, name="ident")
+        warm_in = keep.tile([P, 1], F32, name="warm_in")
+        warm_out = keep.tile([P, 1], F32, name="warm_out")
+
+        nc.vector.memset(planes[:].bitcast(I32), 0)
+        nc.vector.memset(stats[0:MEAN_ROW, :].bitcast(I32), 0)
+        nc.gpsimd.memset(warm_in[:], 0.0)
+
+        nc.sync.dma_start(offsets[:], offs)
+        nc.sync.dma_start(stats[MEAN_ROW : MEAN_ROW + 1, :], mean[0:1, :])
+        nc.sync.dma_start(stats[INV_ROW : INV_ROW + 1, :], inv[0:1, :])
+        for r in range(4):
+            nc.scalar.dma_start(planes[r:P:32, :].bitcast(I32), x_scales[0][r:16:4, :].bitcast(I32))
+        nc.sync.dma_start(w_raw[:], w1.rearrange("(p j) n -> p j n", j=4))
+        nc.sync.dma_start(words[:], x_words[0].rearrange("p n t -> p (n t)").bitcast(I32))
+        nc.scalar.activation(warm_out[:], warm_in[:], ACT.Silu)
+        make_identity(nc, ident[:])
+        nc.scalar.dma_start(gsum_col[:], gsum)
+        nc.scalar.dma_start(b_col[:], b)
+
+        def entries(first, count):
+            return offsets[:, first // 16 : (first + count) // 16]
+
+        gsum_row = psum.tile([P, N], F32, name="gsum_row", tag="y")
+        nc.tensor.transpose(gsum_row[:], gsum_col[:, 0:1].to_broadcast([P, P]), ident[:])
+
+        neg = keep.tile([P, S // BLOCK, 2], F32, name="neg")
+        prod = keep.tile([P, S // BLOCK], F32, name="prod")
+        shift = []
+        for h in range(S // HALF):
+            turned = psum.tile([P, HALF // BLOCK, P], F32, name="turned", tag="fin")
+            for u in range(HALF // STAGE):
+                picked = ring.tile([P, STAGE], F32, name="picked", tag="slot%d" % h, align_bytes=64)
+                nc.vector.tensor_copy(picked[:], stats[:].indirect(entries(h * HALF + u * STAGE, STAGE)))
+                for i in range(STAGE // BLOCK):
+                    nc.tensor.transpose(turned[:, u * (STAGE // BLOCK) + i, :], picked[:, i * BLOCK : (i + 1) * BLOCK], ident[:])
+            blocks = range(h * HALF // BLOCK, (h + 1) * HALF // BLOCK)
+            nc.scalar.activation(neg[:, blocks.start : blocks.stop, :], turned[:, :, MEAN_ROW : INV_ROW + 1], ACT.Copy, scale=-1.0)
+            for k in blocks:
+                nc.scalar.activation(prod[:, k : k + 1], neg[:, k, 0:1], ACT.Copy, scale=neg[:, k, 1:2])
+            for k in blocks:
+                term = keep.tile([P, N], F32, name="term%d" % k)
+                nc.scalar.activation(term[:], gsum_row[:], ACT.Copy, scale=prod[:, k : k + 1])
+                shift.append(term)
+
+        w_bf = keep.tile([P, N, 4], BF16, name="w_bf", align_bytes=64)
+        w_codes = keep.tile([P, N], U32, name="w_codes", align_bytes=64)
+        w_bytes = keep.tile([P, N], U8, name="w_bytes", align_bytes=64)
+        nc.scalar.copy(w_bf[:], w_raw[:].rearrange("p j n -> p n j"))
+        nc.vector.quantize_mx(out=w_codes[:].bitcast(FP8X4), scales=w_bytes[:], in_=w_bf[:].rearrange("p n j -> p (n j)"))
+
+        last = S // STAGE - 1
+        for s in range(S // STAGE):
+            x_bytes = ring.tile([P, STAGE], U8, name="x_bytes", tag="slot0", align_bytes=64)
+            nc.vector.tensor_copy(x_bytes[:], planes[:].indirect(entries(s * STAGE, STAGE)))
+            codes = ring.tile([P, STAGE], U32, name="codes", tag="slot1", align_bytes=64)
+            nc.vector.tensor_copy(codes[:], words[:].bitcast(U32).indirect(entries(s * STAGE, STAGE)))
+            fin = psum.tile([P, STAGE], F32, name="fin", tag="fin")
+            per = STAGE // BLOCK
+            for i in range(per):
+                nc.tensor.matmul(fin[:, i * BLOCK : (i + 1) * BLOCK], shift[s * per + i][:], ident[:], is_transpose=True, start=(i == 0), stop=False)
+            scaled = []
+            for i in range(per):
+                k = s * per + i
+                y = psum.tile([P, N], F32, name="y", tag="y")
+                nc.tensor.matmul_mx(
+                    out=y[:],
+                    lhsT=codes[:, i * BLOCK : (i + 1) * BLOCK].bitcast(FP8X4),
+                    lhsT_scale=x_bytes[:, i * BLOCK : (i + 1) * BLOCK],
+                    rhs=w_codes[:].bitcast(FP8X4),
+                    rhs_scale=w_bytes[:],
+                    start=True,
+                    stop=True,
+                )
+                z = keep.tile([P, N], F32, name="z%d" % k)
+                if s == last and i == 0:
+                    nc.vector.tensor_scalar(z[:], y[:], neg[:, k, 1:2], None, ALU.mult)
+                else:
+                    nc.scalar.activation(z[:], y[:], ACT.Copy, scale=neg[:, k, 1:2])
+                scaled.append(z)
+            for i in range(per):
+                nc.tensor.matmul(fin[:, i * BLOCK : (i + 1) * BLOCK], scaled[i][:], ident[:], is_transpose=True, start=False, stop=(i == per - 1))
+            res = keep.tile([P, STAGE], F32, name="res%d" % s)
+            nc.scalar.activation(res[:], fin[:], ACT.Silu, bias=b_col[:], scale=-1.0)
+            nc.sync.dma_start(out[:, s * STAGE : (s + 1) * STAGE], res[:])

@@ -48,15 +48,15 @@ def tile_picked_lnfold_silu_p_kernel(tc, x_words, x_scales, mean, inv, gsum, b, 
 
         nc.sync.dma_start(offsets[:], offs)
         nc.sync.dma_start(stats[MEAN_ROW : MEAN_ROW + 1, :], mean[0:1, :])
-        nc.sync.dma_start(stats[INV_ROW : INV_ROW + 1, :], inv[0:1, :])
+        nc.scalar.dma_start(stats[INV_ROW : INV_ROW + 1, :], inv[0:1, :])
+        nc.sync.dma_start(gsum_col[:], gsum)
         for r in range(4):
             nc.scalar.dma_start(planes[r:P:32, :].bitcast(I32), x_scales[0][r:16:4, :].bitcast(I32))
         nc.sync.dma_start(w_raw[:], w1.rearrange("(p j) n -> p j n", j=4))
         nc.sync.dma_start(words[:], x_words[0].rearrange("p n t -> p (n t)").bitcast(I32))
         nc.scalar.activation(warm_out[:], warm_in[:], ACT.Silu)
         make_identity(nc, ident[:])
-        nc.scalar.dma_start(gsum_col[:], gsum)
-        nc.scalar.dma_start(b_col[:], b)
+        nc.sync.dma_start(b_col[:], b)
 
         def entries(first, count):
             return offsets[:, first // 16 : (first + count) // 16]
@@ -95,11 +95,15 @@ def tile_picked_lnfold_silu_p_kernel(tc, x_words, x_scales, mean, inv, gsum, b, 
             nc.vector.tensor_copy(x_bytes[:], planes[:].indirect(entries(s * STAGE, STAGE)))
             codes = ring.tile([P, STAGE], U32, name="codes", tag="slot1", align_bytes=64)
             nc.vector.tensor_copy(codes[:], words[:].bitcast(U32).indirect(entries(s * STAGE, STAGE)))
-            fin = psum.tile([P, STAGE], F32, name="fin", tag="fin")
             per = STAGE // BLOCK
-            for i in range(per):
-                nc.tensor.matmul(fin[:, i * BLOCK : (i + 1) * BLOCK], shift[s * per + i][:], ident[:], is_transpose=True, start=(i == 0), stop=False)
-            scaled = []
+            groups = [[s * per + i] for i in range(per)] if s == last else [[s * per + i for i in range(per)]]
+            banks = []
+            for group in groups:
+                fin = psum.tile([P, len(group) * BLOCK], F32, name="fin", tag="fin")
+                for i, k in enumerate(group):
+                    nc.tensor.matmul(fin[:, i * BLOCK : (i + 1) * BLOCK], shift[k][:], ident[:], is_transpose=True, start=(i == 0), stop=False)
+                banks.append(fin)
+            scaled = {}
             for i in range(per):
                 k = s * per + i
                 y = psum.tile([P, N], F32, name="y", tag="y")
@@ -113,13 +117,14 @@ def tile_picked_lnfold_silu_p_kernel(tc, x_words, x_scales, mean, inv, gsum, b, 
                     stop=True,
                 )
                 z = keep.tile([P, N], F32, name="z%d" % k)
-                if s == last and i == 0:
+                if s == last:
                     nc.vector.tensor_scalar(z[:], y[:], neg[:, k, 1:2], None, ALU.mult)
                 else:
                     nc.scalar.activation(z[:], y[:], ACT.Copy, scale=neg[:, k, 1:2])
-                scaled.append(z)
-            for i in range(per):
-                nc.tensor.matmul(fin[:, i * BLOCK : (i + 1) * BLOCK], scaled[i][:], ident[:], is_transpose=True, start=False, stop=(i == per - 1))
-            res = keep.tile([P, STAGE], F32, name="res%d" % s)
-            nc.scalar.activation(res[:], fin[:], ACT.Silu, bias=b_col[:], scale=-1.0)
-            nc.sync.dma_start(out[:, s * STAGE : (s + 1) * STAGE], res[:])
+                scaled[k] = z
+            for fin, group in zip(banks, groups):
+                for i, k in enumerate(group):
+                    nc.tensor.matmul(fin[:, i * BLOCK : (i + 1) * BLOCK], scaled[k][:], ident[:], is_transpose=True, start=False, stop=(i == len(group) - 1))
+                res = keep.tile([P, len(group) * BLOCK], F32, name="res%d" % group[0])
+                nc.scalar.activation(res[:], fin[:], ACT.Silu, bias=b_col[:], scale=-1.0)
+                nc.sync.dma_start(out[:, group[0] * BLOCK : (group[-1] + 1) * BLOCK], res[:])

@@ -28,8 +28,8 @@ def tile_picked_lnfold_silu_p_kernel(tc, x_words, x_scales, mean, inv, gsum, b, 
     nc = tc.nc
     with ExitStack() as ctx:
         keep = ctx.enter_context(tc.tile_pool(name="keep", bufs=1))
-        ring = ctx.enter_context(tc.tile_pool(name="ring", bufs=2))
-        psum = ctx.enter_context(tc.psum_pool(name="psum", bufs=4))
+        shared = ctx.enter_context(tc.tile_pool(name="shared", bufs=1))
+        psum = ctx.enter_context(tc.psum_pool(name="psum", bufs=1))
 
         offsets = keep.tile([P, S // 16], U16, name="offsets")
         stats = keep.tile([P, T], F32, name="stats")
@@ -61,70 +61,100 @@ def tile_picked_lnfold_silu_p_kernel(tc, x_words, x_scales, mean, inv, gsum, b, 
         def entries(first, count):
             return offsets[:, first // 16 : (first + count) // 16]
 
-        gsum_row = psum.tile([P, N], F32, name="gsum_row", tag="y")
-        nc.tensor.transpose(gsum_row[:], gsum_col[:, 0:1].to_broadcast([P, P]), ident[:])
+        per = STAGE // BLOCK
+        stages = S // STAGE
+        last = stages - 1
+        turned_blocks = last * per
+
+        w_slot = shared.tile([P, 4, 4 * N], BF16, name="w_slot", align_bytes=64, offset=4 * S)
+        w_bf = w_slot[:, 0, :]
+        nc.scalar.copy(w_bf.rearrange("p (n j) -> p n j", j=4), w_raw[:].rearrange("p j n -> p n j"))
 
         neg = keep.tile([P, S // BLOCK, 2], F32, name="neg")
-        prod = keep.tile([P, S // BLOCK], F32, name="prod")
-        shift = []
+        prod = keep.tile([P, turned_blocks], F32, name="prod")
+        fins = []
         for h in range(S // HALF):
-            turned = psum.tile([P, HALF // BLOCK, P], F32, name="turned", tag="fin")
-            for u in range(HALF // STAGE):
-                picked = ring.tile([P, STAGE], F32, name="picked", tag="slot%d" % h, align_bytes=64)
-                nc.vector.tensor_copy(picked[:], stats[:].indirect(entries(h * HALF + u * STAGE, STAGE)))
-                for i in range(STAGE // BLOCK):
-                    nc.tensor.transpose(turned[:, u * (STAGE // BLOCK) + i, :], picked[:, i * BLOCK : (i + 1) * BLOCK], ident[:])
-            blocks = range(h * HALF // BLOCK, (h + 1) * HALF // BLOCK)
-            nc.scalar.activation(neg[:, blocks.start : blocks.stop, :], turned[:, :, MEAN_ROW : INV_ROW + 1], ACT.Copy, scale=-1.0)
+            gsum_row = psum.tile([P, N], F32, name="gsum_row%d" % h, tag="y%d" % h)
+            turned = psum.tile([P, HALF // BLOCK, P], F32, name="turned%d" % h, tag="turn%d" % h)
+            picked = shared.tile([P, HALF], F32, name="picked%d" % h, align_bytes=64, offset=4 * HALF * h)
+            nc.vector.tensor_copy(picked[:], stats[:].indirect(entries(h * HALF, HALF)))
+            for i in range(HALF // BLOCK):
+                nc.tensor.transpose(turned[:, i, :], picked[:, i * BLOCK : (i + 1) * BLOCK], ident[:])
+            nc.tensor.transpose(gsum_row[:], gsum_col[:, 0:1].to_broadcast([P, P]), ident[:])
+            first = h * HALF // BLOCK
+            nc.scalar.activation(neg[:, first : first + HALF // BLOCK, :], turned[:, :, MEAN_ROW : INV_ROW + 1], ACT.Copy, scale=-1.0)
+            blocks = range(first, min(first + HALF // BLOCK, turned_blocks))
             for k in blocks:
                 nc.scalar.activation(prod[:, k : k + 1], neg[:, k, 0:1], ACT.Copy, scale=neg[:, k, 1:2])
             for k in blocks:
                 term = keep.tile([P, N], F32, name="term%d" % k)
                 nc.scalar.activation(term[:], gsum_row[:], ACT.Copy, scale=prod[:, k : k + 1])
-                shift.append(term)
+                if k % per == 0:
+                    fin = psum.tile([P, STAGE], F32, name="fin%d" % (k // per), tag=("fin0", "fin1", "turn0")[k // per])
+                    fins.append(fin)
+                i = k % per
+                nc.tensor.matmul(fin[:, i * BLOCK : (i + 1) * BLOCK], term[:], ident[:], is_transpose=True, start=(i == 0), stop=False)
 
-        w_bf = keep.tile([P, N, 4], BF16, name="w_bf", align_bytes=64)
-        w_codes = keep.tile([P, N], U32, name="w_codes", align_bytes=64)
-        w_bytes = keep.tile([P, N], U8, name="w_bytes", align_bytes=64)
-        nc.scalar.copy(w_bf[:], w_raw[:].rearrange("p j n -> p n j"))
-        nc.vector.quantize_mx(out=w_codes[:].bitcast(FP8X4), scales=w_bytes[:], in_=w_bf[:].rearrange("p n j -> p (n j)"))
-
-        last = S // STAGE - 1
-        for s in range(S // STAGE):
-            x_bytes = ring.tile([P, STAGE], U8, name="x_bytes", tag="slot0", align_bytes=64)
-            nc.vector.tensor_copy(x_bytes[:], planes[:].indirect(entries(s * STAGE, STAGE)))
-            codes = ring.tile([P, STAGE], U32, name="codes", tag="slot1", align_bytes=64)
-            nc.vector.tensor_copy(codes[:], words[:].bitcast(U32).indirect(entries(s * STAGE, STAGE)))
-            per = STAGE // BLOCK
-            groups = [[s * per + i] for i in range(per)] if s == last else [[s * per + i for i in range(per)]]
-            banks = []
-            for group in groups:
-                fin = psum.tile([P, len(group) * BLOCK], F32, name="fin", tag="fin")
-                for i, k in enumerate(group):
-                    nc.tensor.matmul(fin[:, i * BLOCK : (i + 1) * BLOCK], shift[k][:], ident[:], is_transpose=True, start=(i == 0), stop=False)
-                banks.append(fin)
-            scaled = {}
+        spread = psum.tile([P, 2, STAGE], F32, name="spread", tag="turn1")
+        for c in range(2):
             for i in range(per):
-                k = s * per + i
-                y = psum.tile([P, N], F32, name="y", tag="y")
+                nc.tensor.transpose(spread[:, c, i * BLOCK : (i + 1) * BLOCK], neg[:, turned_blocks + i, c : c + 1].to_broadcast([P, P]), ident[:])
+        neg_mean = keep.tile([P, STAGE], F32, name="neg_mean")
+        nc.scalar.copy(neg_mean[:], spread[:, 0, :])
+
+        w_codes = shared.tile([P, N], U32, name="w_codes", align_bytes=64, offset=5 * STAGE)
+        w_bytes = keep.tile([P, N], U8, name="w_bytes", align_bytes=64)
+
+        for s in range(stages):
+            place = 0 if s == 0 else 4 * S + 5 * STAGE * (s - 1)
+            x_bytes = shared.tile([P, STAGE], U8, name="x_bytes%d" % s, align_bytes=64, offset=place)
+            nc.vector.tensor_copy(x_bytes[:], planes[:].indirect(entries(s * STAGE, STAGE)))
+            if s == 0:
+                nc.vector.quantize_mx(out=w_codes[:].bitcast(FP8X4), scales=w_bytes[:], in_=w_bf)
+            codes = shared.tile([P, STAGE], U32, name="codes%d" % s, align_bytes=64, offset=place + STAGE)
+            nc.vector.tensor_copy(codes[:], words[:].bitcast(U32).indirect(entries(s * STAGE, STAGE)))
+            if s < last:
+                y = psum.tile([P, per, N], F32, name="y%d" % s, tag="y%d" % (s % 2))
+                for i in range(per):
+                    nc.tensor.matmul_mx(
+                        out=y[:, i, :],
+                        lhsT=codes[:, i * BLOCK : (i + 1) * BLOCK].bitcast(FP8X4),
+                        lhsT_scale=x_bytes[:, i * BLOCK : (i + 1) * BLOCK],
+                        rhs=w_codes[:].bitcast(FP8X4),
+                        rhs_scale=w_bytes[:],
+                        start=True,
+                        stop=True,
+                    )
+                fin = fins[s]
+                for i in range(per):
+                    k = s * per + i
+                    z = keep.tile([P, N], F32, name="z%d" % k)
+                    nc.scalar.activation(z[:], y[:, i, :], ACT.Copy, scale=neg[:, k, 1:2])
+                    nc.tensor.matmul(fin[:, i * BLOCK : (i + 1) * BLOCK], z[:], ident[:], is_transpose=True, start=False, stop=(i == per - 1))
+                res = keep.tile([P, STAGE], F32, name="res%d" % s)
+                nc.scalar.activation(res[:], fin[:], ACT.Silu, bias=b_col[:], scale=-1.0)
+                nc.sync.dma_start(out[:, s * STAGE : (s + 1) * STAGE], res[:])
+            else:
+                y = psum.tile([P, STAGE], F32, name="y%d" % s, tag="y%d" % (s % 2))
                 nc.tensor.matmul_mx(
                     out=y[:],
-                    lhsT=codes[:, i * BLOCK : (i + 1) * BLOCK].bitcast(FP8X4),
-                    lhsT_scale=x_bytes[:, i * BLOCK : (i + 1) * BLOCK],
-                    rhs=w_codes[:].bitcast(FP8X4),
-                    rhs_scale=w_bytes[:],
+                    lhsT=w_codes[:].bitcast(FP8X4),
+                    lhsT_scale=w_bytes[:],
+                    rhs=codes[:].bitcast(FP8X4),
+                    rhs_scale=x_bytes[:],
                     start=True,
                     stop=True,
                 )
-                z = keep.tile([P, N], F32, name="z%d" % k)
-                if s == last:
-                    nc.vector.tensor_scalar(z[:], y[:], neg[:, k, 1:2], None, ALU.mult)
-                else:
-                    nc.scalar.activation(z[:], y[:], ACT.Copy, scale=neg[:, k, 1:2])
-                scaled[k] = z
-            for fin, group in zip(banks, groups):
-                for i, k in enumerate(group):
-                    nc.tensor.matmul(fin[:, i * BLOCK : (i + 1) * BLOCK], scaled[k][:], ident[:], is_transpose=True, start=False, stop=(i == len(group) - 1))
-                res = keep.tile([P, len(group) * BLOCK], F32, name="res%d" % group[0])
-                nc.scalar.activation(res[:], fin[:], ACT.Silu, bias=b_col[:], scale=-1.0)
-                nc.sync.dma_start(out[:, group[0] * BLOCK : (group[-1] + 1) * BLOCK], res[:])
+                centred = []
+                for i in range(per):
+                    cols = slice(i * BLOCK, (i + 1) * BLOCK)
+                    t = keep.tile([P, BLOCK], F32, name="centred%d" % i)
+                    nc.vector.scalar_tensor_tensor(t[:], neg_mean[:, cols], gsum_col[:, 0:1], y[:, cols], ALU.mult, ALU.add)
+                    centred.append(t)
+                for i in range(per):
+                    cols = slice(i * BLOCK, (i + 1) * BLOCK)
+                    u = keep.tile([P, BLOCK], F32, name="scaled%d" % i)
+                    nc.vector.tensor_tensor(u[:], centred[i][:], spread[:, 1, cols], ALU.mult)
+                    res = keep.tile([P, BLOCK], F32, name="res_last%d" % i)
+                    nc.scalar.activation(res[:], u[:], ACT.Silu, bias=b_col[:], scale=-1.0)
+                    nc.sync.dma_start(out[:, s * STAGE + i * BLOCK : s * STAGE + (i + 1) * BLOCK], res[:])

@@ -42,12 +42,12 @@ def tile_picked_lnfold_silu_p_kernel(tc, x_words, x_scales, mean, inv, gsum, b, 
         warm_in = keep.tile([P, 1], F32, name="warm_in")
         warm_out = keep.tile([P, 1], F32, name="warm_out")
 
+        nc.vector.memset(warm_in[:], 0.0)
         nc.vector.memset(planes[:].bitcast(I32), 0)
-        nc.vector.memset(stats[0:MEAN_ROW, :].bitcast(I32), 0)
-        nc.gpsimd.memset(warm_in[:], 0.0)
+        nc.vector.tensor_copy(stats[0:MEAN_ROW, :], warm_in[0:MEAN_ROW, 0:1].to_broadcast([MEAN_ROW, T]))
 
-        nc.sync.dma_start(offsets[:], offs)
         nc.sync.dma_start(stats[MEAN_ROW : MEAN_ROW + 1, :], mean[0:1, :])
+        nc.sync.dma_start(offsets[:], offs)
         nc.scalar.dma_start(stats[INV_ROW : INV_ROW + 1, :], inv[0:1, :])
         nc.sync.dma_start(gsum_col[:], gsum)
         for r in range(4):
@@ -102,16 +102,22 @@ def tile_picked_lnfold_silu_p_kernel(tc, x_words, x_scales, mean, inv, gsum, b, 
         neg_mean = keep.tile([P, STAGE], F32, name="neg_mean")
         nc.scalar.copy(neg_mean[:], spread[:, 0, :])
 
-        w_codes = shared.tile([P, N], U32, name="w_codes", align_bytes=64, offset=5 * STAGE)
+        w_codes = shared.tile([P, N], U32, name="w_codes", align_bytes=64, offset=6 * STAGE)
         w_bytes = keep.tile([P, N], U8, name="w_bytes", align_bytes=64)
 
         for s in range(stages):
-            place = 0 if s == 0 else 4 * S + 5 * STAGE * (s - 1)
-            x_bytes = shared.tile([P, STAGE], U8, name="x_bytes%d" % s, align_bytes=64, offset=place)
-            nc.vector.tensor_copy(x_bytes[:], planes[:].indirect(entries(s * STAGE, STAGE)))
+            place = 4 * S + 5 * STAGE * (s - 1)
             if s == 0:
+                early_bytes = shared.tile([P, HALF], U8, name="early_bytes", align_bytes=64, offset=0)
+                nc.vector.tensor_copy(early_bytes[:], planes[:].indirect(entries(0, HALF)))
                 nc.vector.quantize_mx(out=w_codes[:].bitcast(FP8X4), scales=w_bytes[:], in_=w_bf)
-            codes = shared.tile([P, STAGE], U32, name="codes%d" % s, align_bytes=64, offset=place + STAGE)
+            if s * STAGE < HALF:
+                x_bytes = early_bytes[:, s * STAGE : (s + 1) * STAGE]
+            else:
+                late_bytes = shared.tile([P, STAGE], U8, name="late_bytes%d" % s, align_bytes=64, offset=place)
+                nc.vector.tensor_copy(late_bytes[:], planes[:].indirect(entries(s * STAGE, STAGE)))
+                x_bytes = late_bytes[:]
+            codes = shared.tile([P, STAGE], U32, name="codes%d" % s, align_bytes=64, offset=HALF if s == 0 else place + STAGE)
             nc.vector.tensor_copy(codes[:], words[:].bitcast(U32).indirect(entries(s * STAGE, STAGE)))
             if s < last:
                 y = psum.tile([P, per, N], F32, name="y%d" % s, tag="y%d" % (s % 2))
@@ -141,7 +147,7 @@ def tile_picked_lnfold_silu_p_kernel(tc, x_words, x_scales, mean, inv, gsum, b, 
                     lhsT=w_codes[:].bitcast(FP8X4),
                     lhsT_scale=w_bytes[:],
                     rhs=codes[:].bitcast(FP8X4),
-                    rhs_scale=x_bytes[:],
+                    rhs_scale=x_bytes,
                     start=True,
                     stop=True,
                 )

@@ -46,13 +46,14 @@ def tile_picked_lnfold_silu_p_kernel(tc, x_words, x_scales, mean, inv, gsum, b, 
         nc.vector.memset(planes[:].bitcast(I32), 0)
         nc.vector.tensor_copy(stats[0:MEAN_ROW, :], warm_in[0:MEAN_ROW, 0:1].to_broadcast([MEAN_ROW, T]))
 
-        nc.sync.dma_start(stats[MEAN_ROW : MEAN_ROW + 1, :], mean[0:1, :])
         nc.sync.dma_start(offsets[:], offs)
+        nc.sync.dma_start(stats[MEAN_ROW : MEAN_ROW + 1, :], mean[0:1, :])
         nc.scalar.dma_start(stats[INV_ROW : INV_ROW + 1, :], inv[0:1, :])
         nc.sync.dma_start(gsum_col[:], gsum)
-        for r in range(4):
+        for r in range(3):
             nc.scalar.dma_start(planes[r:P:32, :].bitcast(I32), x_scales[0][r:16:4, :].bitcast(I32))
         nc.sync.dma_start(w_raw[:], w1.rearrange("(p j) n -> p j n", j=4))
+        nc.sync.dma_start(planes[3:P:32, :].bitcast(I32), x_scales[0][3:16:4, :].bitcast(I32))
         nc.sync.dma_start(words[:], x_words[0].rearrange("p n t -> p (n t)").bitcast(I32))
         nc.scalar.activation(warm_out[:], warm_in[:], ACT.Silu)
         make_identity(nc, ident[:])

@@ -44,6 +44,7 @@ def tile_picked_lnfold_silu_p_kernel(tc, x_words, x_scales, mean, inv, gsum, b, 
 
         nc.vector.memset(warm_in[:], 0.0)
         nc.vector.memset(planes[:].bitcast(I32), 0)
+        nc.vector.memset(ident[:], 0.0)
         nc.vector.tensor_copy(stats[0:MEAN_ROW, :], warm_in[0:MEAN_ROW, 0:1].to_broadcast([MEAN_ROW, T]))
 
         nc.sync.dma_start(offsets[:], offs)
@@ -56,7 +57,7 @@ def tile_picked_lnfold_silu_p_kernel(tc, x_words, x_scales, mean, inv, gsum, b, 
         nc.sync.dma_start(planes[3:P:32, :].bitcast(I32), x_scales[0][3:16:4, :].bitcast(I32))
         nc.sync.dma_start(words[:], x_words[0].rearrange("p n t -> p (n t)").bitcast(I32))
         nc.scalar.activation(warm_out[:], warm_in[:], ACT.Silu)
-        make_identity(nc, ident[:])
+        make_identity(nc, ident[:], nomemset=True)
         nc.sync.dma_start(b_col[:], b)
 
         def entries(first, count):
@@ -74,6 +75,8 @@ def tile_picked_lnfold_silu_p_kernel(tc, x_words, x_scales, mean, inv, gsum, b, 
         neg = keep.tile([P, S // BLOCK, 2], F32, name="neg")
         prod = keep.tile([P, turned_blocks], F32, name="prod")
         fins = []
+        pairs = []
+        paired_blocks = turned_blocks - per
         for h in range(S // HALF):
             gsum_row = psum.tile([P, N], F32, name="gsum_row%d" % h, tag="y%d" % h)
             turned = psum.tile([P, HALF // BLOCK, P], F32, name="turned%d" % h, tag="turn%d" % h)
@@ -90,11 +93,16 @@ def tile_picked_lnfold_silu_p_kernel(tc, x_words, x_scales, mean, inv, gsum, b, 
             for k in blocks:
                 term = keep.tile([P, N], F32, name="term%d" % k)
                 nc.scalar.activation(term[:], gsum_row[:], ACT.Copy, scale=prod[:, k : k + 1])
-                if k % per == 0:
-                    fin = psum.tile([P, STAGE], F32, name="fin%d" % (k // per), tag=("fin0", "fin1", "turn0")[k // per])
-                    fins.append(fin)
                 i = k % per
-                nc.tensor.matmul(fin[:, i * BLOCK : (i + 1) * BLOCK], term[:], ident[:], is_transpose=True, start=(i == 0), stop=False)
+                if k >= paired_blocks:
+                    fin = psum.tile([P, BLOCK], F32, name="fin_single%d" % i, tag=("turn0", "single")[i])
+                    fins.append(fin[:])
+                else:
+                    if i == 0:
+                        fin = psum.tile([P, STAGE], F32, name="fin%d" % (k // per), tag="fin%d" % (k // per))
+                        pairs.append(fin)
+                    fins.append(fin[:, i * BLOCK : (i + 1) * BLOCK])
+                nc.tensor.matmul(fins[k], term[:], ident[:], is_transpose=True, start=(i == 0 or k >= paired_blocks), stop=False)
 
         spread = psum.tile([P, 2, STAGE], F32, name="spread", tag="turn1")
         for c in range(2):
@@ -122,9 +130,10 @@ def tile_picked_lnfold_silu_p_kernel(tc, x_words, x_scales, mean, inv, gsum, b, 
             nc.vector.tensor_copy(codes[:], words[:].bitcast(U32).indirect(entries(s * STAGE, STAGE)))
             if s < last:
                 y = psum.tile([P, per, N], F32, name="y%d" % s, tag="y%d" % (s % 2))
+                ys = [y[:, i, :] for i in range(per)]
                 for i in range(per):
                     nc.tensor.matmul_mx(
-                        out=y[:, i, :],
+                        out=ys[i],
                         lhsT=codes[:, i * BLOCK : (i + 1) * BLOCK].bitcast(FP8X4),
                         lhsT_scale=x_bytes[:, i * BLOCK : (i + 1) * BLOCK],
                         rhs=w_codes[:].bitcast(FP8X4),
@@ -132,14 +141,17 @@ def tile_picked_lnfold_silu_p_kernel(tc, x_words, x_scales, mean, inv, gsum, b, 
                         start=True,
                         stop=True,
                     )
-                fin = fins[s]
+                res = keep.tile([P, STAGE], F32, name="res%d" % s)
                 for i in range(per):
                     k = s * per + i
                     z = keep.tile([P, N], F32, name="z%d" % k)
-                    nc.scalar.activation(z[:], y[:, i, :], ACT.Copy, scale=neg[:, k, 1:2])
-                    nc.tensor.matmul(fin[:, i * BLOCK : (i + 1) * BLOCK], z[:], ident[:], is_transpose=True, start=False, stop=(i == per - 1))
-                res = keep.tile([P, STAGE], F32, name="res%d" % s)
-                nc.scalar.activation(res[:], fin[:], ACT.Silu, bias=b_col[:], scale=-1.0)
+                    nc.scalar.activation(z[:], ys[i], ACT.Copy, scale=neg[:, k, 1:2])
+                    nc.tensor.matmul(fins[k], z[:], ident[:], is_transpose=True, start=False, stop=(i == per - 1 or k >= paired_blocks))
+                if s < last - 1:
+                    nc.scalar.activation(res[:], pairs[s][:], ACT.Silu, bias=b_col[:], scale=-1.0)
+                else:
+                    for i in range(per):
+                        nc.scalar.activation(res[:, i * BLOCK : (i + 1) * BLOCK], fins[s * per + i], ACT.Silu, bias=b_col[:], scale=-1.0)
                 nc.sync.dma_start(out[:, s * STAGE : (s + 1) * STAGE], res[:])
             else:
                 y = psum.tile([P, STAGE], F32, name="y%d" % s, tag="y%d" % (s % 2))

@@ -22,6 +22,7 @@ MEAN_ROW, INV_ROW = 126, 127
 HALF = 512
 STAGE = 256
 BLOCK = 128
+BLOCKS = S // BLOCK
 
 
 def tile_picked_lnfold_silu_p_kernel(tc, x_words, x_scales, mean, inv, gsum, b, w1, offs, out):
@@ -33,147 +34,113 @@ def tile_picked_lnfold_silu_p_kernel(tc, x_words, x_scales, mean, inv, gsum, b, 
 
         offsets = keep.tile([P, S // 16], U16, name="offsets")
         stats = keep.tile([P, T], F32, name="stats")
-        words = keep.tile([P, T], I32, name="words", align_bytes=64)
         planes = keep.tile([P, T], U8, name="planes", align_bytes=64)
-        w_raw = keep.tile([P, 4, N], F32, name="w_raw")
+        words = keep.tile([P, T], I32, name="words", align_bytes=64)
+        ident = keep.tile([P, P], F32, name="ident")
+        zero = keep.tile([P, 1], F32, name="zero")
+        warm_out = keep.tile([P, 1], F32, name="warm_out")
         gsum_col = keep.tile([P, 1], F32, name="gsum_col")
         b_col = keep.tile([P, 1], F32, name="b_col")
-        ident = keep.tile([P, P], F32, name="ident")
-        warm_in = keep.tile([P, 1], F32, name="warm_in")
-        warm_out = keep.tile([P, 1], F32, name="warm_out")
+        w_raw_slot = shared.tile([P, 3, 4 * N], F32, name="w_raw_slot", align_bytes=64, offset=0)
+        w_raw = w_raw_slot[:, 0, :]
 
-        nc.vector.memset(warm_in[:], 0.0)
         nc.vector.memset(planes[:].bitcast(I32), 0)
+        nc.vector.memset(zero[:], 0.0)
         nc.vector.memset(ident[:], 0.0)
-        nc.vector.tensor_copy(stats[0:MEAN_ROW, :], warm_in[0:MEAN_ROW, 0:1].to_broadcast([MEAN_ROW, T]))
+        nc.vector.tensor_copy(stats[0:MEAN_ROW, :], zero[0:MEAN_ROW, 0:1].to_broadcast([MEAN_ROW, T]))
+
+        def scale_rows(queue, r):
+            queue.dma_start(planes[r:P:32, :].bitcast(I32), x_scales[0][r:16:4, :].bitcast(I32))
 
         nc.sync.dma_start(offsets[:], offs)
-        nc.sync.dma_start(stats[MEAN_ROW : MEAN_ROW + 1, :], mean[0:1, :])
         nc.scalar.dma_start(stats[INV_ROW : INV_ROW + 1, :], inv[0:1, :])
-        nc.sync.dma_start(gsum_col[:], gsum)
-        for r in range(3):
-            nc.scalar.dma_start(planes[r:P:32, :].bitcast(I32), x_scales[0][r:16:4, :].bitcast(I32))
-        nc.sync.dma_start(w_raw[:], w1.rearrange("(p j) n -> p j n", j=4))
-        nc.sync.dma_start(planes[3:P:32, :].bitcast(I32), x_scales[0][3:16:4, :].bitcast(I32))
+        nc.sync.dma_start(stats[MEAN_ROW : MEAN_ROW + 1, :], mean[0:1, :])
+        for r in range(2):
+            scale_rows(nc.scalar, r)
+            scale_rows(nc.sync, 2 + r)
         nc.sync.dma_start(words[:], x_words[0].rearrange("p n t -> p (n t)").bitcast(I32))
-        nc.scalar.activation(warm_out[:], warm_in[:], ACT.Silu)
+        nc.scalar.activation(warm_out[:], zero[:], ACT.Silu)
         make_identity(nc, ident[:], nomemset=True)
+        nc.sync.dma_start(gsum_col[:], gsum)
         nc.sync.dma_start(b_col[:], b)
+        nc.sync.dma_start(w_raw, w1.rearrange("(p j) n -> p (j n)", j=4))
 
         def entries(first, count):
             return offsets[:, first // 16 : (first + count) // 16]
 
-        per = STAGE // BLOCK
-        stages = S // STAGE
-        last = stages - 1
-        turned_blocks = last * per
-
-        w_slot = shared.tile([P, 4, 4 * N], BF16, name="w_slot", align_bytes=64, offset=4 * S)
-        w_bf = w_slot[:, 0, :]
-        nc.scalar.copy(w_bf.rearrange("p (n j) -> p n j", j=4), w_raw[:].rearrange("p j n -> p n j"))
-
-        neg = keep.tile([P, S // BLOCK, 2], F32, name="neg")
-        prod = keep.tile([P, turned_blocks], F32, name="prod")
-        fins = []
-        pairs = []
-        paired_blocks = turned_blocks - per
+        per_half = HALF // BLOCK
+        gsum_row = psum.tile([P, N], F32, name="gsum_row", tag="gsum")
+        turned = []
         for h in range(S // HALF):
-            gsum_row = psum.tile([P, N], F32, name="gsum_row%d" % h, tag="y%d" % h)
-            turned = psum.tile([P, HALF // BLOCK, P], F32, name="turned%d" % h, tag="turn%d" % h)
-            picked = shared.tile([P, HALF], F32, name="picked%d" % h, align_bytes=64, offset=4 * HALF * h)
-            nc.vector.tensor_copy(picked[:], stats[:].indirect(entries(h * HALF, HALF)))
-            for i in range(HALF // BLOCK):
-                nc.tensor.transpose(turned[:, i, :], picked[:, i * BLOCK : (i + 1) * BLOCK], ident[:])
-            nc.tensor.transpose(gsum_row[:], gsum_col[:, 0:1].to_broadcast([P, P]), ident[:])
-            first = h * HALF // BLOCK
-            nc.scalar.activation(neg[:, first : first + HALF // BLOCK, :], turned[:, :, MEAN_ROW : INV_ROW + 1], ACT.Copy, scale=-1.0)
-            blocks = range(first, min(first + HALF // BLOCK, turned_blocks))
-            for k in blocks:
-                nc.scalar.activation(prod[:, k : k + 1], neg[:, k, 0:1], ACT.Copy, scale=neg[:, k, 1:2])
-            for k in blocks:
-                term = keep.tile([P, N], F32, name="term%d" % k)
-                nc.scalar.activation(term[:], gsum_row[:], ACT.Copy, scale=prod[:, k : k + 1])
-                i = k % per
-                if k >= paired_blocks:
-                    fin = psum.tile([P, BLOCK], F32, name="fin_single%d" % i, tag=("turn0", "single")[i])
-                    fins.append(fin[:])
-                else:
-                    if i == 0:
-                        fin = psum.tile([P, STAGE], F32, name="fin%d" % (k // per), tag="fin%d" % (k // per))
-                        pairs.append(fin)
-                    fins.append(fin[:, i * BLOCK : (i + 1) * BLOCK])
-                nc.tensor.matmul(fins[k], term[:], ident[:], is_transpose=True, start=(i == 0 or k >= paired_blocks), stop=False)
+            picked = keep.tile([P, HALF], F32, name="picked%d" % h)
+            nc.scalar.activation(picked[:], stats[:].indirect(entries(h * HALF, HALF)), ACT.Copy)
+            bank = psum.tile([P, per_half, P], F32, name="turned%d" % h, tag="turn%d" % h)
+            for i in range(per_half):
+                nc.tensor.transpose(bank[:, i, :], picked[:, i * BLOCK : (i + 1) * BLOCK], ident[:])
+            if h == 0:
+                nc.tensor.transpose(gsum_row[:], gsum_col[:, 0:1].to_broadcast([P, P]), ident[:])
+            turned.append(bank)
 
-        spread = psum.tile([P, 2, STAGE], F32, name="spread", tag="turn1")
-        for c in range(2):
-            for i in range(per):
-                nc.tensor.transpose(spread[:, c, i * BLOCK : (i + 1) * BLOCK], neg[:, turned_blocks + i, c : c + 1].to_broadcast([P, P]), ident[:])
-        neg_mean = keep.tile([P, STAGE], F32, name="neg_mean")
-        nc.scalar.copy(neg_mean[:], spread[:, 0, :])
-
-        w_codes = shared.tile([P, N], U32, name="w_codes", align_bytes=64, offset=6 * STAGE)
+        w_slot = shared.tile([P, 2, 4 * N], BF16, name="w_slot", align_bytes=64, offset=48 * N)
+        w_bf = w_slot[:, 0, :]
+        w_codes = keep.tile([P, N], U32, name="w_codes", align_bytes=64)
         w_bytes = keep.tile([P, N], U8, name="w_bytes", align_bytes=64)
 
-        for s in range(stages):
-            place = 4 * S + 5 * STAGE * (s - 1)
-            if s == 0:
-                early_bytes = shared.tile([P, HALF], U8, name="early_bytes", align_bytes=64, offset=0)
-                nc.vector.tensor_copy(early_bytes[:], planes[:].indirect(entries(0, HALF)))
+        negs = []
+        terms = []
+        for h in range(S // HALF):
+            if h == 0:
+                neg = keep.tile([P, per_half, 2], F32, name="neg0")
+            else:
+                neg = shared.tile([P, per_half, 2], F32, name="neg1", offset=4 * N * BLOCKS)
+            prod = keep.tile([P, per_half], F32, name="prod%d" % h)
+            nc.scalar.activation(neg[:], turned[h][:, :, MEAN_ROW : INV_ROW + 1], ACT.Copy, scale=-1.0)
+            if h == 0:
+                nc.scalar.copy(w_bf.rearrange("p (n j) -> p n j", j=4), w_raw.rearrange("p (j n) -> p n j", j=4))
+            for i in range(per_half):
+                nc.scalar.activation(prod[:, i : i + 1], neg[:, i, 0:1], ACT.Copy, scale=neg[:, i, 1:2])
+            for i in range(per_half):
+                k = h * per_half + i
+                term = shared.tile([P, N], F32, name="term%d" % k, offset=4 * N * k)
+                nc.scalar.activation(term[:], gsum_row[:], ACT.Copy, scale=prod[:, i : i + 1])
+                terms.append(term)
+                negs.append(neg[:, i, 1:2])
+
+        x_bytes = keep.tile([P, S], U8, name="x_bytes", align_bytes=64)
+        nc.vector.tensor_copy(x_bytes[:], planes[:].indirect(offsets[:]))
+        codes = []
+        for s in range(S // STAGE):
+            if s < 2:
+                part = keep.tile([P, STAGE], U32, name="codes%d" % s, align_bytes=64)
+            else:
+                part = shared.tile([P, STAGE], U32, name="codes%d" % s, align_bytes=64, offset=48 * N + 4 * STAGE * (s - 2))
+            nc.vector.tensor_copy(part[:], words[:].bitcast(U32).indirect(entries(s * STAGE, STAGE)))
+            codes.append(part)
+            if s == 1:
                 nc.vector.quantize_mx(out=w_codes[:].bitcast(FP8X4), scales=w_bytes[:], in_=w_bf)
-            if s * STAGE < HALF:
-                x_bytes = early_bytes[:, s * STAGE : (s + 1) * STAGE]
-            else:
-                late_bytes = shared.tile([P, STAGE], U8, name="late_bytes%d" % s, align_bytes=64, offset=place)
-                nc.vector.tensor_copy(late_bytes[:], planes[:].indirect(entries(s * STAGE, STAGE)))
-                x_bytes = late_bytes[:]
-            codes = shared.tile([P, STAGE], U32, name="codes%d" % s, align_bytes=64, offset=HALF if s == 0 else place + STAGE)
-            nc.vector.tensor_copy(codes[:], words[:].bitcast(U32).indirect(entries(s * STAGE, STAGE)))
-            if s < last:
-                y = psum.tile([P, per, N], F32, name="y%d" % s, tag="y%d" % (s % 2))
-                ys = [y[:, i, :] for i in range(per)]
-                for i in range(per):
-                    nc.tensor.matmul_mx(
-                        out=ys[i],
-                        lhsT=codes[:, i * BLOCK : (i + 1) * BLOCK].bitcast(FP8X4),
-                        lhsT_scale=x_bytes[:, i * BLOCK : (i + 1) * BLOCK],
-                        rhs=w_codes[:].bitcast(FP8X4),
-                        rhs_scale=w_bytes[:],
-                        start=True,
-                        stop=True,
-                    )
-                res = keep.tile([P, STAGE], F32, name="res%d" % s)
-                for i in range(per):
-                    k = s * per + i
-                    z = keep.tile([P, N], F32, name="z%d" % k)
-                    nc.scalar.activation(z[:], ys[i], ACT.Copy, scale=neg[:, k, 1:2])
-                    nc.tensor.matmul(fins[k], z[:], ident[:], is_transpose=True, start=False, stop=(i == per - 1 or k >= paired_blocks))
-                if s < last - 1:
-                    nc.scalar.activation(res[:], pairs[s][:], ACT.Silu, bias=b_col[:], scale=-1.0)
-                else:
-                    for i in range(per):
-                        nc.scalar.activation(res[:, i * BLOCK : (i + 1) * BLOCK], fins[s * per + i], ACT.Silu, bias=b_col[:], scale=-1.0)
-                nc.sync.dma_start(out[:, s * STAGE : (s + 1) * STAGE], res[:])
-            else:
-                y = psum.tile([P, STAGE], F32, name="y%d" % s, tag="y%d" % (s % 2))
+
+        ys = []
+        for s, tag in enumerate(("a", "b", "turn0", "turn1")):
+            y = psum.tile([P, 2, N], F32, name="y%d" % s, tag=tag)
+            for i in range(2):
                 nc.tensor.matmul_mx(
-                    out=y[:],
-                    lhsT=w_codes[:].bitcast(FP8X4),
-                    lhsT_scale=w_bytes[:],
-                    rhs=codes[:].bitcast(FP8X4),
-                    rhs_scale=x_bytes,
+                    out=y[:, i, :],
+                    lhsT=codes[s][:, i * BLOCK : (i + 1) * BLOCK].bitcast(FP8X4),
+                    lhsT_scale=x_bytes[:, s * STAGE + i * BLOCK : s * STAGE + (i + 1) * BLOCK],
+                    rhs=w_codes[:].bitcast(FP8X4),
+                    rhs_scale=w_bytes[:],
                     start=True,
                     stop=True,
                 )
-                centred = []
-                for i in range(per):
-                    cols = slice(i * BLOCK, (i + 1) * BLOCK)
-                    t = keep.tile([P, BLOCK], F32, name="centred%d" % i)
-                    nc.vector.scalar_tensor_tensor(t[:], neg_mean[:, cols], gsum_col[:, 0:1], y[:, cols], ALU.mult, ALU.add)
-                    centred.append(t)
-                for i in range(per):
-                    cols = slice(i * BLOCK, (i + 1) * BLOCK)
-                    u = keep.tile([P, BLOCK], F32, name="scaled%d" % i)
-                    nc.vector.tensor_tensor(u[:], centred[i][:], spread[:, 1, cols], ALU.mult)
-                    res = keep.tile([P, BLOCK], F32, name="res_last%d" % i)
-                    nc.scalar.activation(res[:], u[:], ACT.Silu, bias=b_col[:], scale=-1.0)
-                    nc.sync.dma_start(out[:, s * STAGE + i * BLOCK : s * STAGE + (i + 1) * BLOCK], res[:])
+                ys.append(y[:, i, :])
+
+        for s, tag in enumerate(("c", "d", "a", "b")):
+            fin = psum.tile([P, 2, BLOCK], F32, name="fin%d" % s, tag=tag)
+            for i in range(2):
+                k = 2 * s + i
+                v = keep.tile([P, N], F32, name="v%d" % k)
+                nc.vector.scalar_tensor_tensor(v[:], ys[k], negs[k], terms[k][:], ALU.mult, ALU.add)
+                nc.tensor.transpose(fin[:, i, :], v[:], ident[:])
+            res = keep.tile([P, STAGE], F32, name="res%d" % s)
+            nc.scalar.activation(res[:], fin[:].rearrange("p i n -> p (i n)"), ACT.Silu, bias=b_col[:], scale=-1.0)
+            nc.sync.dma_start(out[:, s * STAGE : (s + 1) * STAGE], res[:])

@@ -61,9 +61,12 @@ def tile_picked_lnfold_silu_p_kernel(tc, x_words, x_scales, mean, inv, gsum, b, 
         nc.sync.dma_start(words[:], x_words[0].rearrange("p n t -> p (n t)").bitcast(I32))
         nc.scalar.activation(warm_out[:], zero[:], ACT.Silu)
         make_identity(nc, ident[:], nomemset=True)
+        w_rows = w1.rearrange("(p j) n -> p (j n)", j=4)
+        for half in range(2):
+            cols = slice(half * 2 * N, (half + 1) * 2 * N)
+            nc.sync.dma_start(w_raw[:, cols], w_rows[:, cols])
         nc.sync.dma_start(gsum_col[:], gsum)
         nc.sync.dma_start(b_col[:], b)
-        nc.sync.dma_start(w_raw, w1.rearrange("(p j) n -> p (j n)", j=4))
 
         def entries(first, count):
             return offsets[:, first // 16 : (first + count) // 16]

@@ -55,9 +55,8 @@ def tile_picked_lnfold_silu_p_kernel(tc, x_words, x_scales, mean, inv, gsum, b, 
         nc.sync.dma_start(offsets[:], offs)
         nc.scalar.dma_start(stats[INV_ROW : INV_ROW + 1, :], inv[0:1, :])
         nc.sync.dma_start(stats[MEAN_ROW : MEAN_ROW + 1, :], mean[0:1, :])
-        for r in range(2):
-            scale_rows(nc.scalar, r)
-            scale_rows(nc.sync, 2 + r)
+        for r in range(4):
+            scale_rows(nc.sync, r)
         nc.sync.dma_start(words[:], x_words[0].rearrange("p n t -> p (n t)").bitcast(I32))
         nc.scalar.activation(warm_out[:], zero[:], ACT.Silu)
         make_identity(nc, ident[:], nomemset=True)

@@ -60,18 +60,33 @@ def tile_picked_lnfold_silu_p_kernel(tc, x_words, x_scales, mean, inv, gsum, b, 
         nc.sync.dma_start(words[:], x_words[0].rearrange("p n t -> p (n t)").bitcast(I32))
         nc.scalar.activation(warm_out[:], zero[:], ACT.Silu)
         make_identity(nc, ident[:], nomemset=True)
-        w_rows = w1.rearrange("(p j) n -> p (j n)", j=4)
-        for half in range(2):
-            cols = slice(half * 2 * N, (half + 1) * 2 * N)
-            nc.sync.dma_start(w_raw[:, cols], w_rows[:, cols])
+        nc.sync.dma_start(w_raw, w1.rearrange("(p j) n -> p (j n)", j=4))
         nc.sync.dma_start(gsum_col[:], gsum)
         nc.sync.dma_start(b_col[:], b)
 
         def entries(first, count):
             return offsets[:, first // 16 : (first + count) // 16]
 
+        w_slot = shared.tile([P, 2, 4 * N], BF16, name="w_slot", align_bytes=64, offset=48 * N)
+        w_bf = w_slot[:, 0, :]
+        w_codes = keep.tile([P, N], U32, name="w_codes", align_bytes=64)
+        w_bytes = keep.tile([P, N], U8, name="w_bytes", align_bytes=64)
+        x_bytes = keep.tile([P, S], U8, name="x_bytes", align_bytes=64)
+        nc.vector.tensor_copy(x_bytes[:], planes[:].indirect(offsets[:]))
+        stages = S // STAGE
+        per_stage = STAGE // BLOCK
+        codes = {}
+        for turn, s in enumerate(list(range(1, stages)) + [0]):
+            if turn < 2:
+                codes[s] = keep.tile([P, STAGE], U32, name="codes%d" % s, align_bytes=64)
+            else:
+                codes[s] = shared.tile([P, STAGE], U32, name="codes%d" % s, align_bytes=64, offset=48 * N + 4 * STAGE * (turn - 2))
+            nc.vector.tensor_copy(codes[s][:], words[:].bitcast(U32).indirect(entries(s * STAGE, STAGE)))
+            if turn == 1:
+                nc.scalar.copy(w_bf.rearrange("p (c i j) -> p c j i", i=4, j=4), w_raw.rearrange("p (j c i) -> p c j i", i=4, j=4))
+                nc.vector.quantize_mx(out=w_codes[:].bitcast(FP8X4), scales=w_bytes[:], in_=w_bf)
+
         per_half = HALF // BLOCK
-        gsum_row = psum.tile([P, N], F32, name="gsum_row", tag="gsum")
         turned = []
         for h in range(S // HALF):
             picked = keep.tile([P, HALF], F32, name="picked%d" % h)
@@ -79,54 +94,35 @@ def tile_picked_lnfold_silu_p_kernel(tc, x_words, x_scales, mean, inv, gsum, b, 
             bank = psum.tile([P, per_half, P], F32, name="turned%d" % h, tag="turn%d" % h)
             for i in range(per_half):
                 nc.tensor.transpose(bank[:, i, :], picked[:, i * BLOCK : (i + 1) * BLOCK], ident[:])
-            if h == 0:
-                nc.tensor.transpose(gsum_row[:], gsum_col[:, 0:1].to_broadcast([P, P]), ident[:])
             turned.append(bank)
 
-        w_slot = shared.tile([P, 2, 4 * N], BF16, name="w_slot", align_bytes=64, offset=48 * N)
-        w_bf = w_slot[:, 0, :]
-        w_codes = keep.tile([P, N], U32, name="w_codes", align_bytes=64)
-        w_bytes = keep.tile([P, N], U8, name="w_bytes", align_bytes=64)
-
-        negs = []
-        terms = []
+        negs = [keep.tile([P, per_half, 2], F32, name="neg0"), shared.tile([P, per_half, 2], F32, name="neg1", offset=0)]
+        prods = {s: shared.tile([P, per_stage], F32, name="prod%d" % s, offset=64 * N + 4 * STAGE * (s % 2) * s) for s in range(1, stages)}
+        spread = psum.tile([P, 2, STAGE], F32, name="spread", tag="spread")
         for h in range(S // HALF):
+            first = h * per_half
+            nc.scalar.activation(negs[h][:], turned[h][:, :, MEAN_ROW : INV_ROW + 1], ACT.Copy, scale=-1.0)
             if h == 0:
-                neg = keep.tile([P, per_half, 2], F32, name="neg0")
-            else:
-                neg = shared.tile([P, per_half, 2], F32, name="neg1", offset=4 * N * BLOCKS)
-            prod = keep.tile([P, per_half], F32, name="prod%d" % h)
-            nc.scalar.activation(neg[:], turned[h][:, :, MEAN_ROW : INV_ROW + 1], ACT.Copy, scale=-1.0)
-            if h == 0:
-                nc.scalar.copy(w_bf.rearrange("p (n j) -> p n j", j=4), w_raw.rearrange("p (j n) -> p n j", j=4))
-            for i in range(per_half):
-                nc.scalar.activation(prod[:, i : i + 1], neg[:, i, 0:1], ACT.Copy, scale=neg[:, i, 1:2])
-            for i in range(per_half):
-                k = h * per_half + i
-                term = shared.tile([P, N], F32, name="term%d" % k, offset=4 * N * k)
-                nc.scalar.activation(term[:], gsum_row[:], ACT.Copy, scale=prod[:, i : i + 1])
-                terms.append(term)
-                negs.append(neg[:, i, 1:2])
+                for c in range(2):
+                    for i in range(per_stage):
+                        nc.tensor.transpose(spread[:, c, i * BLOCK : (i + 1) * BLOCK], negs[0][:, i, c : c + 1].to_broadcast([P, P]), ident[:])
+            for k in range(max(first, per_stage), first + per_half):
+                nc.scalar.activation(prods[k // per_stage][:, k % per_stage : k % per_stage + 1], negs[h][:, k - first, 0:1], ACT.Copy, scale=negs[h][:, k - first, 1:2])
+        gsum_row = psum.tile([P, N], F32, name="gsum_row", tag="gsum")
+        nc.tensor.transpose(gsum_row[:], gsum_col[:, 0:1].to_broadcast([P, P]), ident[:])
+        terms = {}
+        for k in range(per_stage, BLOCKS):
+            terms[k] = keep.tile([P, N], F32, name="term%d" % k)
+            nc.scalar.activation(terms[k][:], gsum_row[:], ACT.Copy, scale=prods[k // per_stage][:, k % per_stage : k % per_stage + 1])
+        neg_mean = shared.tile([P, STAGE], F32, name="neg_mean", offset=64 * N)
+        nc.scalar.copy(neg_mean[:], spread[:, 0, :])
 
-        x_bytes = keep.tile([P, S], U8, name="x_bytes", align_bytes=64)
-        nc.vector.tensor_copy(x_bytes[:], planes[:].indirect(offsets[:]))
-        codes = []
-        for s in range(S // STAGE):
-            if s < 2:
-                part = keep.tile([P, STAGE], U32, name="codes%d" % s, align_bytes=64)
-            else:
-                part = shared.tile([P, STAGE], U32, name="codes%d" % s, align_bytes=64, offset=48 * N + 4 * STAGE * (s - 2))
-            nc.vector.tensor_copy(part[:], words[:].bitcast(U32).indirect(entries(s * STAGE, STAGE)))
-            codes.append(part)
-            if s == 1:
-                nc.vector.quantize_mx(out=w_codes[:].bitcast(FP8X4), scales=w_bytes[:], in_=w_bf)
-
-        ys = []
-        for s, tag in enumerate(("a", "b", "turn0", "turn1")):
-            y = psum.tile([P, 2, N], F32, name="y%d" % s, tag=tag)
-            for i in range(2):
+        ys = {}
+        for s, tag in ((1, "a"), (2, "b"), (3, "turn0")):
+            ys[s] = psum.tile([P, per_stage, N], F32, name="y%d" % s, tag=tag)
+            for i in range(per_stage):
                 nc.tensor.matmul_mx(
-                    out=y[:, i, :],
+                    out=ys[s][:, i, :],
                     lhsT=codes[s][:, i * BLOCK : (i + 1) * BLOCK].bitcast(FP8X4),
                     lhsT_scale=x_bytes[:, s * STAGE + i * BLOCK : s * STAGE + (i + 1) * BLOCK],
                     rhs=w_codes[:].bitcast(FP8X4),
@@ -134,15 +130,39 @@ def tile_picked_lnfold_silu_p_kernel(tc, x_words, x_scales, mean, inv, gsum, b, 
                     start=True,
                     stop=True,
                 )
-                ys.append(y[:, i, :])
+        y_last = psum.tile([P, STAGE], F32, name="y_last", tag="turn1")
+        nc.tensor.matmul_mx(
+            out=y_last[:],
+            lhsT=w_codes[:].bitcast(FP8X4),
+            lhsT_scale=w_bytes[:],
+            rhs=codes[0][:].bitcast(FP8X4),
+            rhs_scale=x_bytes[:, 0:STAGE],
+            start=True,
+            stop=True,
+        )
 
-        for s, tag in enumerate(("c", "d", "a", "b")):
-            fin = psum.tile([P, 2, BLOCK], F32, name="fin%d" % s, tag=tag)
-            for i in range(2):
-                k = 2 * s + i
+        def finish(values, first, count):
+            res = keep.tile([P, count], F32, name="res%d" % first)
+            nc.scalar.activation(res[:], values, ACT.Silu, bias=b_col[:], scale=-1.0)
+            nc.sync.dma_start(out[:, first : first + count], res[:])
+
+        for s, tag in ((1, "c"), (2, "d"), (3, "a")):
+            fin = psum.tile([P, per_stage, BLOCK], F32, name="fin%d" % s, tag=tag)
+            for i in range(per_stage):
+                k = per_stage * s + i
                 v = keep.tile([P, N], F32, name="v%d" % k)
-                nc.vector.scalar_tensor_tensor(v[:], ys[k], negs[k], terms[k][:], ALU.mult, ALU.add)
+                nc.vector.scalar_tensor_tensor(v[:], ys[s][:, i, :], negs[k // per_half][:, k % per_half, 1:2], terms[k][:], ALU.mult, ALU.add)
                 nc.tensor.transpose(fin[:, i, :], v[:], ident[:])
-            res = keep.tile([P, STAGE], F32, name="res%d" % s)
-            nc.scalar.activation(res[:], fin[:].rearrange("p i n -> p (i n)"), ACT.Silu, bias=b_col[:], scale=-1.0)
-            nc.sync.dma_start(out[:, s * STAGE : (s + 1) * STAGE], res[:])
+            finish(fin[:].rearrange("p i n -> p (i n)"), s * STAGE, STAGE)
+
+        centred = []
+        for i in range(per_stage):
+            cols = slice(i * BLOCK, (i + 1) * BLOCK)
+            t = keep.tile([P, BLOCK], F32, name="centred%d" % i)
+            nc.vector.scalar_tensor_tensor(t[:], neg_mean[:, cols], gsum_col[:, 0:1], y_last[:, cols], ALU.mult, ALU.add)
+            centred.append(t)
+        for i in range(per_stage):
+            cols = slice(i * BLOCK, (i + 1) * BLOCK)
+            u = keep.tile([P, BLOCK], F32, name="scaled%d" % i)
+            nc.vector.tensor_tensor(u[:], centred[i][:], spread[:, 1, cols], ALU.mult)
+            finish(u[:], i * BLOCK, BLOCK)

@@ -71,6 +71,8 @@ def tile_picked_lnfold_silu_p_kernel(tc, x_words, x_scales, mean, inv, gsum, b, 
         w_bf = w_slot[:, 0, :]
         w_codes = keep.tile([P, N], U32, name="w_codes", align_bytes=64)
         w_bytes = keep.tile([P, N], U8, name="w_bytes", align_bytes=64)
+        picked_first = keep.tile([P, STAGE], F32, name="picked_first")
+        nc.vector.tensor_copy(picked_first[:], stats[:].indirect(entries(0, STAGE)))
         x_bytes = keep.tile([P, S], U8, name="x_bytes", align_bytes=64)
         nc.vector.tensor_copy(x_bytes[:], planes[:].indirect(offsets[:]))
         stages = S // STAGE
@@ -89,11 +91,16 @@ def tile_picked_lnfold_silu_p_kernel(tc, x_words, x_scales, mean, inv, gsum, b, 
         per_half = HALF // BLOCK
         turned = []
         for h in range(S // HALF):
-            picked = keep.tile([P, HALF], F32, name="picked%d" % h)
-            nc.scalar.activation(picked[:], stats[:].indirect(entries(h * HALF, HALF)), ACT.Copy)
+            first = max(h * HALF, STAGE)
+            count = (h + 1) * HALF - first
+            picked = keep.tile([P, count], F32, name="picked%d" % h)
+            nc.scalar.activation(picked[:], stats[:].indirect(entries(first, count)), ACT.Copy)
+            blocks = [picked[:, j : j + BLOCK] for j in range(0, count, BLOCK)]
+            if h == 0:
+                blocks = [picked_first[:, j : j + BLOCK] for j in range(0, STAGE, BLOCK)] + blocks
             bank = psum.tile([P, per_half, P], F32, name="turned%d" % h, tag="turn%d" % h)
             for i in range(per_half):
-                nc.tensor.transpose(bank[:, i, :], picked[:, i * BLOCK : (i + 1) * BLOCK], ident[:])
+                nc.tensor.transpose(bank[:, i, :], blocks[i], ident[:])
             turned.append(bank)
 
         negs = [keep.tile([P, per_half, 2], F32, name="neg0"), shared.tile([P, per_half, 2], F32, name="neg1", offset=0)]

@@ -78,7 +78,7 @@ def tile_picked_lnfold_silu_p_kernel(tc, x_words, x_scales, mean, inv, gsum, b, 
         stages = S // STAGE
         per_stage = STAGE // BLOCK
         codes = {}
-        for turn, s in enumerate(list(range(1, stages)) + [0]):
+        for turn, s in enumerate((1, 2, 0, 3)):
             if turn < 2:
                 codes[s] = keep.tile([P, STAGE], U32, name="codes%d" % s, align_bytes=64)
             else:
@@ -115,61 +115,58 @@ def tile_picked_lnfold_silu_p_kernel(tc, x_words, x_scales, mean, inv, gsum, b, 
                         nc.tensor.transpose(spread[:, c, i * BLOCK : (i + 1) * BLOCK], negs[0][:, i, c : c + 1].to_broadcast([P, P]), ident[:])
             for k in range(max(first, per_stage), first + per_half):
                 nc.scalar.activation(prods[k // per_stage][:, k % per_stage : k % per_stage + 1], negs[h][:, k - first, 0:1], ACT.Copy, scale=negs[h][:, k - first, 1:2])
+        neg_mean = shared.tile([P, STAGE], F32, name="neg_mean", offset=4 * STAGE)
+        nc.scalar.copy(neg_mean[:], spread[:, 0, :])
         gsum_row = psum.tile([P, N], F32, name="gsum_row", tag="gsum")
         nc.tensor.transpose(gsum_row[:], gsum_col[:, 0:1].to_broadcast([P, P]), ident[:])
         terms = {}
         for k in range(per_stage, BLOCKS):
             terms[k] = keep.tile([P, N], F32, name="term%d" % k)
             nc.scalar.activation(terms[k][:], gsum_row[:], ACT.Copy, scale=prods[k // per_stage][:, k % per_stage : k % per_stage + 1])
-        neg_mean = shared.tile([P, STAGE], F32, name="neg_mean", offset=64 * N)
-        nc.scalar.copy(neg_mean[:], spread[:, 0, :])
 
         ys = {}
-        for s, tag in ((1, "a"), (2, "b"), (3, "turn0")):
-            ys[s] = psum.tile([P, per_stage, N], F32, name="y%d" % s, tag=tag)
-            for i in range(per_stage):
+        for s, tag in ((1, "a"), (2, "b"), (0, "turn1"), (3, "turn0")):
+            ys[s] = psum.tile([P, STAGE], F32, name="y%d" % s, tag=tag)
+            tokens = x_bytes[:, s * STAGE : (s + 1) * STAGE]
+            if s == 0:
                 nc.tensor.matmul_mx(
-                    out=ys[s][:, i, :],
-                    lhsT=codes[s][:, i * BLOCK : (i + 1) * BLOCK].bitcast(FP8X4),
-                    lhsT_scale=x_bytes[:, s * STAGE + i * BLOCK : s * STAGE + (i + 1) * BLOCK],
-                    rhs=w_codes[:].bitcast(FP8X4),
-                    rhs_scale=w_bytes[:],
+                    out=ys[s][:],
+                    lhsT=w_codes[:].bitcast(FP8X4),
+                    lhsT_scale=w_bytes[:],
+                    rhs=codes[s][:].bitcast(FP8X4),
+                    rhs_scale=tokens,
                     start=True,
                     stop=True,
                 )
-        y_last = psum.tile([P, STAGE], F32, name="y_last", tag="turn1")
-        nc.tensor.matmul_mx(
-            out=y_last[:],
-            lhsT=w_codes[:].bitcast(FP8X4),
-            lhsT_scale=w_bytes[:],
-            rhs=codes[0][:].bitcast(FP8X4),
-            rhs_scale=x_bytes[:, 0:STAGE],
-            start=True,
-            stop=True,
-        )
+            else:
+                for i in range(per_stage):
+                    cols = slice(i * BLOCK, (i + 1) * BLOCK)
+                    nc.tensor.matmul_mx(
+                        out=ys[s][:, cols],
+                        lhsT=codes[s][:, cols].bitcast(FP8X4),
+                        lhsT_scale=tokens[:, cols],
+                        rhs=w_codes[:].bitcast(FP8X4),
+                        rhs_scale=w_bytes[:],
+                        start=True,
+                        stop=True,
+                    )
 
         def finish(values, first, count):
             res = keep.tile([P, count], F32, name="res%d" % first)
             nc.scalar.activation(res[:], values, ACT.Silu, bias=b_col[:], scale=-1.0)
             nc.sync.dma_start(out[:, first : first + count], res[:])
 
-        for s, tag in ((1, "c"), (2, "d"), (3, "a")):
-            fin = psum.tile([P, per_stage, BLOCK], F32, name="fin%d" % s, tag=tag)
-            for i in range(per_stage):
-                k = per_stage * s + i
+        centred = keep.tile([P, STAGE], F32, name="centred")
+        scaled = keep.tile([P, STAGE], F32, name="scaled")
+        nc.vector.scalar_tensor_tensor(centred[:], neg_mean[:], gsum_col[:, 0:1], ys[0][:], ALU.mult, ALU.add)
+        nc.vector.tensor_tensor(scaled[:], centred[:], spread[:, 1, :], ALU.mult)
+        finish(scaled[:], 0, STAGE)
+        for first, count, tag in ((2, 2, "c"), (4, 2, "d"), (6, 1, "a"), (7, 1, "gsum")):
+            fin = psum.tile([P, count, BLOCK], F32, name="fin%d" % first, tag=tag)
+            for i in range(count):
+                k = first + i
+                cols = slice(k % per_stage * BLOCK, (k % per_stage + 1) * BLOCK)
                 v = keep.tile([P, N], F32, name="v%d" % k)
-                nc.vector.scalar_tensor_tensor(v[:], ys[s][:, i, :], negs[k // per_half][:, k % per_half, 1:2], terms[k][:], ALU.mult, ALU.add)
+                nc.vector.scalar_tensor_tensor(v[:], ys[k // per_stage][:, cols], negs[k // per_half][:, k % per_half, 1:2], terms[k][:], ALU.mult, ALU.add)
                 nc.tensor.transpose(fin[:, i, :], v[:], ident[:])
-            finish(fin[:].rearrange("p i n -> p (i n)"), s * STAGE, STAGE)
-
-        centred = []
-        for i in range(per_stage):
-            cols = slice(i * BLOCK, (i + 1) * BLOCK)
-            t = keep.tile([P, BLOCK], F32, name="centred%d" % i)
-            nc.vector.scalar_tensor_tensor(t[:], neg_mean[:, cols], gsum_col[:, 0:1], y_last[:, cols], ALU.mult, ALU.add)
-            centred.append(t)
-        for i in range(per_stage):
-            cols = slice(i * BLOCK, (i + 1) * BLOCK)
-            u = keep.tile([P, BLOCK], F32, name="scaled%d" % i)
-            nc.vector.tensor_tensor(u[:], centred[i][:], spread[:, 1, cols], ALU.mult)
-            finish(u[:], i * BLOCK, BLOCK)
+            finish(fin[:].rearrange("p i n -> p (i n)"), first * BLOCK, count * BLOCK)

@@ -19,6 +19,7 @@ ACT = mybir.ActivationFunctionType
 ALU = mybir.AluOpType
 
 MEAN_ROW, INV_ROW = 126, 127
+SCALE_FIRST, SCALE_ROWS = 48, 16
 HALF = 512
 STAGE = 256
 BLOCK = 128
@@ -29,144 +30,120 @@ def tile_picked_lnfold_silu_p_kernel(tc, x_words, x_scales, mean, inv, gsum, b, 
     nc = tc.nc
     with ExitStack() as ctx:
         keep = ctx.enter_context(tc.tile_pool(name="keep", bufs=1))
-        shared = ctx.enter_context(tc.tile_pool(name="shared", bufs=1))
         psum = ctx.enter_context(tc.psum_pool(name="psum", bufs=1))
 
         offsets = keep.tile([P, S // 16], U16, name="offsets")
         stats = keep.tile([P, T], F32, name="stats")
-        planes = keep.tile([P, T], U8, name="planes", align_bytes=64)
+        scale_table = keep.tile([P, T], U8, name="scale_table", align_bytes=64)
         words = keep.tile([P, T], I32, name="words", align_bytes=64)
+        x_scale = keep.tile([P, S], U8, name="x_scale", align_bytes=64)
         ident = keep.tile([P, P], F32, name="ident")
         zero = keep.tile([P, 1], F32, name="zero")
         warm_out = keep.tile([P, 1], F32, name="warm_out")
         gsum_col = keep.tile([P, 1], F32, name="gsum_col")
         b_col = keep.tile([P, 1], F32, name="b_col")
-        w_raw_slot = shared.tile([P, 3, 4 * N], F32, name="w_raw_slot", align_bytes=64, offset=0)
-        w_raw = w_raw_slot[:, 0, :]
+        w_raw = keep.tile([P, 4 * N], F32, name="w_raw", align_bytes=64)
 
-        nc.vector.memset(planes[:].bitcast(I32), 0)
+        scale_last = SCALE_FIRST + SCALE_ROWS
         nc.vector.memset(zero[:], 0.0)
-        nc.vector.memset(ident[:], 0.0)
+        nc.vector.memset(scale_table[0:SCALE_FIRST, :].bitcast(I32), 0)
+        nc.vector.memset(scale_table[scale_last:P, :].bitcast(I32), 0)
         nc.vector.tensor_copy(stats[0:MEAN_ROW, :], zero[0:MEAN_ROW, 0:1].to_broadcast([MEAN_ROW, T]))
-
-        def scale_rows(queue, r):
-            queue.dma_start(planes[r:P:32, :].bitcast(I32), x_scales[0][r:16:4, :].bitcast(I32))
+        nc.vector.memset(ident[:], 0.0)
+        nc.vector.memset(x_scale[:].bitcast(I32), 0)
 
         nc.sync.dma_start(offsets[:], offs)
-        nc.scalar.dma_start(stats[INV_ROW : INV_ROW + 1, :], inv[0:1, :])
+        nc.sync.dma_start(scale_table[SCALE_FIRST:scale_last, :].bitcast(I32), x_scales[0].bitcast(I32))
+        nc.scalar.dma_start(gsum_col[:], gsum)
         nc.sync.dma_start(stats[MEAN_ROW : MEAN_ROW + 1, :], mean[0:1, :])
-        for r in range(4):
-            scale_rows(nc.sync, r)
+        nc.sync.dma_start(stats[INV_ROW : INV_ROW + 1, :], inv[0:1, :])
+        nc.sync.dma_start(w_raw[:], w1.rearrange("(p j) n -> p (j n)", j=4))
         nc.sync.dma_start(words[:], x_words[0].rearrange("p n t -> p (n t)").bitcast(I32))
+        nc.sync.dma_start(b_col[:], b)
         nc.scalar.activation(warm_out[:], zero[:], ACT.Silu)
         make_identity(nc, ident[:], nomemset=True)
-        nc.sync.dma_start(w_raw, w1.rearrange("(p j) n -> p (j n)", j=4))
-        nc.sync.dma_start(gsum_col[:], gsum)
-        nc.sync.dma_start(b_col[:], b)
 
         def entries(first, count):
             return offsets[:, first // 16 : (first + count) // 16]
 
-        w_slot = shared.tile([P, 2, 4 * N], BF16, name="w_slot", align_bytes=64, offset=48 * N)
-        w_bf = w_slot[:, 0, :]
+        picked_rows = keep.tile([P, S], U8, name="picked_rows", align_bytes=64)
+        nc.vector.tensor_copy(picked_rows[:], scale_table[:].indirect(offsets[:]))
+        for q in range(4):
+            src = SCALE_FIRST + 4 * q
+            nc.sync.dma_start(x_scale[32 * q : 32 * q + 4, :].bitcast(I32), picked_rows[src : src + 4, :].bitcast(I32))
+
+        w_bf = keep.tile([P, 4 * N], BF16, name="w_bf", align_bytes=64)
         w_codes = keep.tile([P, N], U32, name="w_codes", align_bytes=64)
-        w_bytes = keep.tile([P, N], U8, name="w_bytes", align_bytes=64)
-        picked_first = keep.tile([P, STAGE], F32, name="picked_first")
-        nc.vector.tensor_copy(picked_first[:], stats[:].indirect(entries(0, STAGE)))
-        x_bytes = keep.tile([P, S], U8, name="x_bytes", align_bytes=64)
-        nc.vector.tensor_copy(x_bytes[:], planes[:].indirect(offsets[:]))
-        stages = S // STAGE
+        w_scale = keep.tile([P, N], U8, name="w_scale", align_bytes=64)
+        nc.vector.tensor_copy(w_bf[:].rearrange("p (c i j) -> p c j i", i=4, j=4), w_raw[:].rearrange("p (j c i) -> p c j i", i=4, j=4))
+        nc.vector.quantize_mx(out=w_codes[:].bitcast(FP8X4), scales=w_scale[:], in_=w_bf[:])
+
         per_stage = STAGE // BLOCK
+        order = (1, 2, 3, 0)
         codes = {}
-        for turn, s in enumerate((1, 2, 0, 3)):
-            if turn < 2:
-                codes[s] = keep.tile([P, STAGE], U32, name="codes%d" % s, align_bytes=64)
-            else:
-                codes[s] = shared.tile([P, STAGE], U32, name="codes%d" % s, align_bytes=64, offset=48 * N + 4 * STAGE * (turn - 2))
+        for s in order:
+            codes[s] = keep.tile([P, STAGE], U32, name="codes%d" % s, align_bytes=64)
             nc.vector.tensor_copy(codes[s][:], words[:].bitcast(U32).indirect(entries(s * STAGE, STAGE)))
-            if turn == 1:
-                nc.scalar.copy(w_bf.rearrange("p (c i j) -> p c j i", i=4, j=4), w_raw.rearrange("p (j c i) -> p c j i", i=4, j=4))
-                nc.vector.quantize_mx(out=w_codes[:].bitcast(FP8X4), scales=w_bytes[:], in_=w_bf)
 
         per_half = HALF // BLOCK
         turned = []
         for h in range(S // HALF):
-            first = max(h * HALF, STAGE)
-            count = (h + 1) * HALF - first
-            picked = keep.tile([P, count], F32, name="picked%d" % h)
-            nc.scalar.activation(picked[:], stats[:].indirect(entries(first, count)), ACT.Copy)
-            blocks = [picked[:, j : j + BLOCK] for j in range(0, count, BLOCK)]
-            if h == 0:
-                blocks = [picked_first[:, j : j + BLOCK] for j in range(0, STAGE, BLOCK)] + blocks
+            picked = keep.tile([P, HALF], F32, name="picked%d" % h)
+            nc.scalar.activation(picked[:], stats[:].indirect(entries(h * HALF, HALF)), ACT.Copy)
             bank = psum.tile([P, per_half, P], F32, name="turned%d" % h, tag="turn%d" % h)
             for i in range(per_half):
-                nc.tensor.transpose(bank[:, i, :], blocks[i], ident[:])
+                nc.tensor.transpose(bank[:, i, :], picked[:, i * BLOCK : (i + 1) * BLOCK], ident[:])
             turned.append(bank)
+            if h == 0:
+                gsum_row = psum.tile([P, N], F32, name="gsum_row", tag="gsum")
+                nc.tensor.transpose(gsum_row[:], gsum_col[:, 0:1].to_broadcast([P, P]), ident[:])
 
-        negs = [keep.tile([P, per_half, 2], F32, name="neg0"), shared.tile([P, per_half, 2], F32, name="neg1", offset=0)]
-        prods = {s: shared.tile([P, per_stage], F32, name="prod%d" % s, offset=64 * N + 4 * STAGE * (s % 2) * s) for s in range(1, stages)}
         spread = psum.tile([P, 2, STAGE], F32, name="spread", tag="spread")
+        neg_mean = keep.tile([P, STAGE], F32, name="neg_mean")
+        negs, terms = [], {}
         for h in range(S // HALF):
             first = h * per_half
-            nc.scalar.activation(negs[h][:], turned[h][:, :, MEAN_ROW : INV_ROW + 1], ACT.Copy, scale=-1.0)
+            neg = keep.tile([P, per_half, 2], F32, name="neg%d" % h)
+            negs.append(neg)
+            nc.scalar.activation(neg[:], turned[h][:, :, MEAN_ROW : INV_ROW + 1], ACT.Copy, scale=-1.0)
             if h == 0:
                 for c in range(2):
                     for i in range(per_stage):
-                        nc.tensor.transpose(spread[:, c, i * BLOCK : (i + 1) * BLOCK], negs[0][:, i, c : c + 1].to_broadcast([P, P]), ident[:])
+                        nc.tensor.transpose(spread[:, c, i * BLOCK : (i + 1) * BLOCK], neg[:, i, c : c + 1].to_broadcast([P, P]), ident[:])
+            else:
+                nc.scalar.copy(neg_mean[:], spread[:, 0, :])
             for k in range(max(first, per_stage), first + per_half):
-                nc.scalar.activation(prods[k // per_stage][:, k % per_stage : k % per_stage + 1], negs[h][:, k - first, 0:1], ACT.Copy, scale=negs[h][:, k - first, 1:2])
-        neg_mean = shared.tile([P, STAGE], F32, name="neg_mean", offset=4 * STAGE)
-        nc.scalar.copy(neg_mean[:], spread[:, 0, :])
-        gsum_row = psum.tile([P, N], F32, name="gsum_row", tag="gsum")
-        nc.tensor.transpose(gsum_row[:], gsum_col[:, 0:1].to_broadcast([P, P]), ident[:])
-        terms = {}
-        for k in range(per_stage, BLOCKS):
-            terms[k] = keep.tile([P, N], F32, name="term%d" % k)
-            nc.scalar.activation(terms[k][:], gsum_row[:], ACT.Copy, scale=prods[k // per_stage][:, k % per_stage : k % per_stage + 1])
+                prod = keep.tile([P, 1], F32, name="prod%d" % k)
+                nc.scalar.activation(prod[:], neg[:, k - first, 0:1], ACT.Copy, scale=neg[:, k - first, 1:2])
+                terms[k] = keep.tile([P, N], F32, name="term%d" % k)
+                nc.scalar.activation(terms[k][:], gsum_row[:], ACT.Copy, scale=prod[:])
 
         ys = {}
-        for s, tag in ((1, "a"), (2, "b"), (0, "turn1"), (3, "turn0")):
+        for s, tag in ((1, "a"), (2, "b"), (3, "turn0"), (0, "turn1")):
             ys[s] = psum.tile([P, STAGE], F32, name="y%d" % s, tag=tag)
-            tokens = x_bytes[:, s * STAGE : (s + 1) * STAGE]
+            tokens = x_scale[:, s * STAGE : (s + 1) * STAGE]
             if s == 0:
-                nc.tensor.matmul_mx(
-                    out=ys[s][:],
-                    lhsT=w_codes[:].bitcast(FP8X4),
-                    lhsT_scale=w_bytes[:],
-                    rhs=codes[s][:].bitcast(FP8X4),
-                    rhs_scale=tokens,
-                    start=True,
-                    stop=True,
-                )
+                nc.tensor.matmul_mx(out=ys[s][:], lhsT=w_codes[:].bitcast(FP8X4), lhsT_scale=w_scale[:], rhs=codes[s][:].bitcast(FP8X4), rhs_scale=tokens, start=True, stop=True)
             else:
                 for i in range(per_stage):
                     cols = slice(i * BLOCK, (i + 1) * BLOCK)
-                    nc.tensor.matmul_mx(
-                        out=ys[s][:, cols],
-                        lhsT=codes[s][:, cols].bitcast(FP8X4),
-                        lhsT_scale=tokens[:, cols],
-                        rhs=w_codes[:].bitcast(FP8X4),
-                        rhs_scale=w_bytes[:],
-                        start=True,
-                        stop=True,
-                    )
+                    nc.tensor.matmul_mx(out=ys[s][:, cols], lhsT=codes[s][:, cols].bitcast(FP8X4), lhsT_scale=tokens[:, cols], rhs=w_codes[:].bitcast(FP8X4), rhs_scale=w_scale[:], start=True, stop=True)
 
         def finish(values, first, count):
             res = keep.tile([P, count], F32, name="res%d" % first)
             nc.scalar.activation(res[:], values, ACT.Silu, bias=b_col[:], scale=-1.0)
             nc.sync.dma_start(out[:, first : first + count], res[:])
 
+        for s, tag in ((1, "c"), (2, "d"), (3, "a")):
+            fin = psum.tile([P, per_stage, BLOCK], F32, name="fin%d" % s, tag=tag)
+            for i in range(per_stage):
+                k = s * per_stage + i
+                v = keep.tile([P, N], F32, name="v%d" % k)
+                nc.vector.scalar_tensor_tensor(v[:], ys[s][:, i * BLOCK : (i + 1) * BLOCK], negs[k // per_half][:, k % per_half, 1:2], terms[k][:], ALU.mult, ALU.add)
+                nc.tensor.transpose(fin[:, i, :], v[:], ident[:])
+            finish(fin[:].rearrange("p i n -> p (i n)"), s * STAGE, STAGE)
         centred = keep.tile([P, STAGE], F32, name="centred")
         scaled = keep.tile([P, STAGE], F32, name="scaled")
         nc.vector.scalar_tensor_tensor(centred[:], neg_mean[:], gsum_col[:, 0:1], ys[0][:], ALU.mult, ALU.add)
         nc.vector.tensor_tensor(scaled[:], centred[:], spread[:, 1, :], ALU.mult)
         finish(scaled[:], 0, STAGE)
-        for first, count, tag in ((2, 2, "c"), (4, 2, "d"), (6, 1, "a"), (7, 1, "gsum")):
-            fin = psum.tile([P, count, BLOCK], F32, name="fin%d" % first, tag=tag)
-            for i in range(count):
-                k = first + i
-                cols = slice(k % per_stage * BLOCK, (k % per_stage + 1) * BLOCK)
-                v = keep.tile([P, N], F32, name="v%d" % k)
-                nc.vector.scalar_tensor_tensor(v[:], ys[k // per_stage][:, cols], negs[k // per_half][:, k % per_half, 1:2], terms[k][:], ALU.mult, ALU.add)
-                nc.tensor.transpose(fin[:, i, :], v[:], ident[:])
-            finish(fin[:].rearrange("p i n -> p (i n)"), first * BLOCK, count * BLOCK)

@@ -19,7 +19,7 @@ ACT = mybir.ActivationFunctionType
 ALU = mybir.AluOpType
 
 MEAN_ROW, INV_ROW = 126, 127
-SCALE_FIRST, SCALE_ROWS = 48, 16
+SCALE_FIRST, SCALE_ROWS = 112, 16
 HALF = 512
 STAGE = 256
 BLOCK = 128
@@ -30,10 +30,11 @@ def tile_picked_lnfold_silu_p_kernel(tc, x_words, x_scales, mean, inv, gsum, b, 
     nc = tc.nc
     with ExitStack() as ctx:
         keep = ctx.enter_context(tc.tile_pool(name="keep", bufs=1))
+        shared = ctx.enter_context(tc.tile_pool(name="shared", bufs=1))
         psum = ctx.enter_context(tc.psum_pool(name="psum", bufs=1))
 
         offsets = keep.tile([P, S // 16], U16, name="offsets")
-        stats = keep.tile([P, T], F32, name="stats")
+        stats = shared.tile([P, T], F32, name="stats", offset=16 * N)
         scale_table = keep.tile([P, T], U8, name="scale_table", align_bytes=64)
         words = keep.tile([P, T], I32, name="words", align_bytes=64)
         x_scale = keep.tile([P, S], U8, name="x_scale", align_bytes=64)
@@ -42,23 +43,22 @@ def tile_picked_lnfold_silu_p_kernel(tc, x_words, x_scales, mean, inv, gsum, b, 
         warm_out = keep.tile([P, 1], F32, name="warm_out")
         gsum_col = keep.tile([P, 1], F32, name="gsum_col")
         b_col = keep.tile([P, 1], F32, name="b_col")
-        w_raw = keep.tile([P, 4 * N], F32, name="w_raw", align_bytes=64)
+        w_raw = shared.tile([P, 4 * N], F32, name="w_raw", align_bytes=64, offset=0)
 
         scale_last = SCALE_FIRST + SCALE_ROWS
         nc.vector.memset(zero[:], 0.0)
-        nc.vector.memset(scale_table[0:SCALE_FIRST, :].bitcast(I32), 0)
-        nc.vector.memset(scale_table[scale_last:P, :].bitcast(I32), 0)
-        nc.vector.tensor_copy(stats[0:MEAN_ROW, :], zero[0:MEAN_ROW, 0:1].to_broadcast([MEAN_ROW, T]))
         nc.vector.memset(ident[:], 0.0)
-        nc.vector.memset(x_scale[:].bitcast(I32), 0)
+        nc.vector.memset(scale_table[0:SCALE_FIRST, :].bitcast(I32), 0)
+        nc.vector.tensor_copy(stats[0:MEAN_ROW, :], zero[0:MEAN_ROW, 0:1].to_broadcast([MEAN_ROW, T]))
+        nc.gpsimd.memset(x_scale[:].bitcast(I32), 0)
 
         nc.sync.dma_start(offsets[:], offs)
         nc.sync.dma_start(scale_table[SCALE_FIRST:scale_last, :].bitcast(I32), x_scales[0].bitcast(I32))
-        nc.scalar.dma_start(gsum_col[:], gsum)
-        nc.sync.dma_start(stats[MEAN_ROW : MEAN_ROW + 1, :], mean[0:1, :])
-        nc.sync.dma_start(stats[INV_ROW : INV_ROW + 1, :], inv[0:1, :])
-        nc.sync.dma_start(w_raw[:], w1.rearrange("(p j) n -> p (j n)", j=4))
+        nc.scalar.dma_start(stats[MEAN_ROW : MEAN_ROW + 1, :], mean[0:1, :])
+        nc.scalar.dma_start(stats[INV_ROW : INV_ROW + 1, :], inv[0:1, :])
         nc.sync.dma_start(words[:], x_words[0].rearrange("p n t -> p (n t)").bitcast(I32))
+        nc.sync.dma_start(w_raw[:], w1.rearrange("(p j) n -> p (j n)", j=4))
+        nc.sync.dma_start(gsum_col[:], gsum)
         nc.sync.dma_start(b_col[:], b)
         nc.scalar.activation(warm_out[:], zero[:], ACT.Silu)
         make_identity(nc, ident[:], nomemset=True)
@@ -72,18 +72,20 @@ def tile_picked_lnfold_silu_p_kernel(tc, x_words, x_scales, mean, inv, gsum, b, 
             src = SCALE_FIRST + 4 * q
             nc.sync.dma_start(x_scale[32 * q : 32 * q + 4, :].bitcast(I32), picked_rows[src : src + 4, :].bitcast(I32))
 
-        w_bf = keep.tile([P, 4 * N], BF16, name="w_bf", align_bytes=64)
+        w_bf = shared.tile([P, 4 * N], BF16, name="w_bf", align_bytes=64, offset=16 * N)
         w_codes = keep.tile([P, N], U32, name="w_codes", align_bytes=64)
         w_scale = keep.tile([P, N], U8, name="w_scale", align_bytes=64)
-        nc.vector.tensor_copy(w_bf[:].rearrange("p (c i j) -> p c j i", i=4, j=4), w_raw[:].rearrange("p (j c i) -> p c j i", i=4, j=4))
-        nc.vector.quantize_mx(out=w_codes[:].bitcast(FP8X4), scales=w_scale[:], in_=w_bf[:])
 
         per_stage = STAGE // BLOCK
         order = (1, 2, 3, 0)
         codes = {}
-        for s in order:
-            codes[s] = keep.tile([P, STAGE], U32, name="codes%d" % s, align_bytes=64)
+
+        def gather_words(s, pool, **place):
+            codes[s] = pool.tile([P, STAGE], U32, name="codes%d" % s, align_bytes=64, **place)
             nc.vector.tensor_copy(codes[s][:], words[:].bitcast(U32).indirect(entries(s * STAGE, STAGE)))
+
+        for s in order[:-1]:
+            gather_words(s, keep)
 
         per_half = HALF // BLOCK
         turned = []
@@ -94,29 +96,35 @@ def tile_picked_lnfold_silu_p_kernel(tc, x_words, x_scales, mean, inv, gsum, b, 
             for i in range(per_half):
                 nc.tensor.transpose(bank[:, i, :], picked[:, i * BLOCK : (i + 1) * BLOCK], ident[:])
             turned.append(bank)
-            if h == 0:
-                gsum_row = psum.tile([P, N], F32, name="gsum_row", tag="gsum")
-                nc.tensor.transpose(gsum_row[:], gsum_col[:, 0:1].to_broadcast([P, P]), ident[:])
 
+        gsum_row = psum.tile([P, N], F32, name="gsum_row", tag="gsum")
+        nc.tensor.transpose(gsum_row[:], gsum_col[:, 0:1].to_broadcast([P, P]), ident[:])
         spread = psum.tile([P, 2, STAGE], F32, name="spread", tag="spread")
-        neg_mean = keep.tile([P, STAGE], F32, name="neg_mean")
-        negs, terms = [], {}
+        neg_mean = shared.tile([P, STAGE], F32, name="neg_mean", offset=4 * STAGE)
+        negs, prods, terms = [], {}, {}
         for h in range(S // HALF):
             first = h * per_half
-            neg = keep.tile([P, per_half, 2], F32, name="neg%d" % h)
+            if h == 0:
+                neg = keep.tile([P, per_half, 2], F32, name="neg0")
+            else:
+                neg = shared.tile([P, per_half, 2], F32, name="neg1", offset=0)
             negs.append(neg)
             nc.scalar.activation(neg[:], turned[h][:, :, MEAN_ROW : INV_ROW + 1], ACT.Copy, scale=-1.0)
             if h == 0:
                 for c in range(2):
                     for i in range(per_stage):
                         nc.tensor.transpose(spread[:, c, i * BLOCK : (i + 1) * BLOCK], neg[:, i, c : c + 1].to_broadcast([P, P]), ident[:])
-            else:
-                nc.scalar.copy(neg_mean[:], spread[:, 0, :])
             for k in range(max(first, per_stage), first + per_half):
-                prod = keep.tile([P, 1], F32, name="prod%d" % k)
-                nc.scalar.activation(prod[:], neg[:, k - first, 0:1], ACT.Copy, scale=neg[:, k - first, 1:2])
-                terms[k] = keep.tile([P, N], F32, name="term%d" % k)
-                nc.scalar.activation(terms[k][:], gsum_row[:], ACT.Copy, scale=prod[:])
+                prods[k] = keep.tile([P, 1], F32, name="prod%d" % k)
+                nc.scalar.activation(prods[k][:], neg[:, k - first, 0:1], ACT.Copy, scale=neg[:, k - first, 1:2])
+            if h == 0:
+                nc.scalar.copy(w_bf[:].rearrange("p (c i j) -> p c j i", i=4, j=4), w_raw[:].rearrange("p (j c i) -> p c j i", i=4, j=4))
+                nc.vector.quantize_mx(out=w_codes[:].bitcast(FP8X4), scales=w_scale[:], in_=w_bf[:])
+                gather_words(order[-1], shared, offset=16 * N)
+        for k in range(per_stage, BLOCKS):
+            terms[k] = keep.tile([P, N], F32, name="term%d" % k)
+            nc.scalar.activation(terms[k][:], gsum_row[:], ACT.Copy, scale=prods[k][:])
+        nc.scalar.copy(neg_mean[:], spread[:, 0, :])
 
         ys = {}
         for s, tag in ((1, "a"), (2, "b"), (3, "turn0"), (0, "turn1")):
@@ -134,16 +142,17 @@ def tile_picked_lnfold_silu_p_kernel(tc, x_words, x_scales, mean, inv, gsum, b, 
             nc.scalar.activation(res[:], values, ACT.Silu, bias=b_col[:], scale=-1.0)
             nc.sync.dma_start(out[:, first : first + count], res[:])
 
+        centred = keep.tile([P, STAGE], F32, name="centred")
+        scaled = keep.tile([P, STAGE], F32, name="scaled")
         for s, tag in ((1, "c"), (2, "d"), (3, "a")):
             fin = psum.tile([P, per_stage, BLOCK], F32, name="fin%d" % s, tag=tag)
             for i in range(per_stage):
                 k = s * per_stage + i
                 v = keep.tile([P, N], F32, name="v%d" % k)
+                if k == BLOCKS - 1:
+                    nc.vector.scalar_tensor_tensor(centred[:], neg_mean[:], gsum_col[:, 0:1], ys[0][:], ALU.mult, ALU.add)
                 nc.vector.scalar_tensor_tensor(v[:], ys[s][:, i * BLOCK : (i + 1) * BLOCK], negs[k // per_half][:, k % per_half, 1:2], terms[k][:], ALU.mult, ALU.add)
                 nc.tensor.transpose(fin[:, i, :], v[:], ident[:])
             finish(fin[:].rearrange("p i n -> p (i n)"), s * STAGE, STAGE)
-        centred = keep.tile([P, STAGE], F32, name="centred")
-        scaled = keep.tile([P, STAGE], F32, name="scaled")
-        nc.vector.scalar_tensor_tensor(centred[:], neg_mean[:], gsum_col[:, 0:1], ys[0][:], ALU.mult, ALU.add)
         nc.vector.tensor_tensor(scaled[:], centred[:], spread[:, 1, :], ALU.mult)
         finish(scaled[:], 0, STAGE)

@@ -52,8 +52,8 @@ def tile_picked_lnfold_silu_p_kernel(tc, x_words, x_scales, mean, inv, gsum, b, 
         nc.vector.tensor_copy(stats[0:MEAN_ROW, :], zero[0:MEAN_ROW, 0:1].to_broadcast([MEAN_ROW, T]))
         nc.gpsimd.memset(x_scale[:].bitcast(I32), 0)
 
-        nc.sync.dma_start(offsets[:], offs)
         nc.sync.dma_start(scale_table[SCALE_FIRST:scale_last, :].bitcast(I32), x_scales[0].bitcast(I32))
+        nc.sync.dma_start(offsets[:], offs)
         nc.scalar.dma_start(stats[MEAN_ROW : MEAN_ROW + 1, :], mean[0:1, :])
         nc.scalar.dma_start(stats[INV_ROW : INV_ROW + 1, :], inv[0:1, :])
         nc.sync.dma_start(words[:], x_words[0].rearrange("p n t -> p (n t)").bitcast(I32))
@@ -77,15 +77,16 @@ def tile_picked_lnfold_silu_p_kernel(tc, x_words, x_scales, mean, inv, gsum, b, 
         w_scale = keep.tile([P, N], U8, name="w_scale", align_bytes=64)
 
         per_stage = STAGE // BLOCK
-        order = (1, 2, 3, 0)
         codes = {}
 
-        def gather_words(s, pool, **place):
-            codes[s] = pool.tile([P, STAGE], U32, name="codes%d" % s, align_bytes=64, **place)
-            nc.vector.tensor_copy(codes[s][:], words[:].bitcast(U32).indirect(entries(s * STAGE, STAGE)))
+        def gather_words(first, count, pool, **place):
+            piece = pool.tile([P, count], U32, name="codes%d" % first, align_bytes=64, **place)
+            nc.vector.tensor_copy(piece[:], words[:].bitcast(U32).indirect(entries(first, count)))
+            for k in range(first // BLOCK, (first + count) // BLOCK):
+                codes[k] = piece[:, k * BLOCK - first : (k + 1) * BLOCK - first]
+            return piece
 
-        for s in order[:-1]:
-            gather_words(s, keep)
+        gather_words(STAGE, S - STAGE - BLOCK, keep)
 
         per_half = HALF // BLOCK
         turned = []
@@ -114,13 +115,14 @@ def tile_picked_lnfold_silu_p_kernel(tc, x_words, x_scales, mean, inv, gsum, b, 
                 for c in range(2):
                     for i in range(per_stage):
                         nc.tensor.transpose(spread[:, c, i * BLOCK : (i + 1) * BLOCK], neg[:, i, c : c + 1].to_broadcast([P, P]), ident[:])
-            for k in range(max(first, per_stage), first + per_half):
-                prods[k] = keep.tile([P, 1], F32, name="prod%d" % k)
-                nc.scalar.activation(prods[k][:], neg[:, k - first, 0:1], ACT.Copy, scale=neg[:, k - first, 1:2])
             if h == 0:
                 nc.scalar.copy(w_bf[:].rearrange("p (c i j) -> p c j i", i=4, j=4), w_raw[:].rearrange("p (j c i) -> p c j i", i=4, j=4))
                 nc.vector.quantize_mx(out=w_codes[:].bitcast(FP8X4), scales=w_scale[:], in_=w_bf[:])
-                gather_words(order[-1], shared, offset=16 * N)
+                gather_words(S - BLOCK, BLOCK, shared, offset=16 * N)
+                wide_codes = gather_words(0, STAGE, shared, offset=16 * N + 4 * BLOCK)
+            for k in range(max(first, per_stage), first + per_half):
+                prods[k] = shared.tile([P, 1], F32, name="prod%d" % k, offset=64 + 32 * k)
+                nc.scalar.activation(prods[k][:], neg[:, k - first, 0:1], ACT.Copy, scale=neg[:, k - first, 1:2])
         for k in range(per_stage, BLOCKS):
             terms[k] = keep.tile([P, N], F32, name="term%d" % k)
             nc.scalar.activation(terms[k][:], gsum_row[:], ACT.Copy, scale=prods[k][:])
@@ -131,11 +133,11 @@ def tile_picked_lnfold_silu_p_kernel(tc, x_words, x_scales, mean, inv, gsum, b, 
             ys[s] = psum.tile([P, STAGE], F32, name="y%d" % s, tag=tag)
             tokens = x_scale[:, s * STAGE : (s + 1) * STAGE]
             if s == 0:
-                nc.tensor.matmul_mx(out=ys[s][:], lhsT=w_codes[:].bitcast(FP8X4), lhsT_scale=w_scale[:], rhs=codes[s][:].bitcast(FP8X4), rhs_scale=tokens, start=True, stop=True)
+                nc.tensor.matmul_mx(out=ys[s][:], lhsT=w_codes[:].bitcast(FP8X4), lhsT_scale=w_scale[:], rhs=wide_codes[:].bitcast(FP8X4), rhs_scale=tokens, start=True, stop=True)
             else:
                 for i in range(per_stage):
                     cols = slice(i * BLOCK, (i + 1) * BLOCK)
-                    nc.tensor.matmul_mx(out=ys[s][:, cols], lhsT=codes[s][:, cols].bitcast(FP8X4), lhsT_scale=tokens[:, cols], rhs=w_codes[:].bitcast(FP8X4), rhs_scale=w_scale[:], start=True, stop=True)
+                    nc.tensor.matmul_mx(out=ys[s][:, cols], lhsT=codes[s * per_stage + i].bitcast(FP8X4), lhsT_scale=tokens[:, cols], rhs=w_codes[:].bitcast(FP8X4), rhs_scale=w_scale[:], start=True, stop=True)
 
         def finish(values, first, count):
             res = keep.tile([P, count], F32, name="res%d" % first)

from contextlib import ExitStack

import concourse.mybir as mybir
from concourse.masks import make_identity

K, T, S, N = 512, 2048, 1024, 128
P = 128
FLOPS = 2 * K * N * S
BYTES = K * T + (K // 32) * T + 2 * 4 * T + 4 * K * N + 2 * 4 * N + 2 * P * (S // 16) + 4 * N * S

F32 = mybir.dt.float32
BF16 = mybir.dt.bfloat16
I32 = mybir.dt.int32
U32 = mybir.dt.uint32
U16 = mybir.dt.uint16
U8 = mybir.dt.uint8
FP8X4 = mybir.dt.float8_e4m3fn_x4
ACT = mybir.ActivationFunctionType
ALU = mybir.AluOpType

MEAN_ROW, INV_ROW = 126, 127
SCALE_FIRST, SCALE_ROWS = 112, 16
HALF = 512
STAGE = 256
BLOCK = 128
BLOCKS = S // BLOCK


def tile_picked_lnfold_silu_p_kernel(tc, x_words, x_scales, mean, inv, gsum, b, w1, offs, out):
    nc = tc.nc
    with ExitStack() as ctx:
        keep = ctx.enter_context(tc.tile_pool(name="keep", bufs=1))
        shared = ctx.enter_context(tc.tile_pool(name="shared", bufs=1))
        psum = ctx.enter_context(tc.psum_pool(name="psum", bufs=1))

        offsets = keep.tile([P, S // 16], U16, name="offsets")
        stats = shared.tile([P, T], F32, name="stats", offset=16 * N)
        scale_table = keep.tile([P, T], U8, name="scale_table", align_bytes=64)
        words = keep.tile([P, T], I32, name="words", align_bytes=64)
        x_scale = keep.tile([P, S], U8, name="x_scale", align_bytes=64)
        ident = keep.tile([P, P], F32, name="ident")
        zero = keep.tile([P, 1], F32, name="zero")
        warm_out = keep.tile([P, 1], F32, name="warm_out")
        gsum_col = keep.tile([P, 1], F32, name="gsum_col")
        b_col = keep.tile([P, 1], F32, name="b_col")
        w_raw = shared.tile([P, 4 * N], F32, name="w_raw", align_bytes=64, offset=0)

        scale_last = SCALE_FIRST + SCALE_ROWS
        nc.vector.memset(zero[:], 0.0)
        nc.vector.memset(ident[:], 0.0)
        nc.vector.memset(scale_table[0:SCALE_FIRST, :].bitcast(I32), 0)
        nc.vector.tensor_copy(stats[0:MEAN_ROW, :], zero[0:MEAN_ROW, 0:1].to_broadcast([MEAN_ROW, T]))
        nc.gpsimd.memset(x_scale[:].bitcast(I32), 0)

        nc.sync.dma_start(scale_table[SCALE_FIRST:scale_last, :].bitcast(I32), x_scales[0].bitcast(I32))
        nc.sync.dma_start(offsets[:], offs)
        nc.scalar.dma_start(stats[MEAN_ROW : MEAN_ROW + 1, :], mean[0:1, :])
        nc.scalar.dma_start(stats[INV_ROW : INV_ROW + 1, :], inv[0:1, :])
        nc.sync.dma_start(words[:], x_words[0].rearrange("p n t -> p (n t)").bitcast(I32))
        nc.sync.dma_start(w_raw[:], w1.rearrange("(p j) n -> p (j n)", j=4))
        nc.sync.dma_start(gsum_col[:], gsum)
        nc.sync.dma_start(b_col[:], b)
        nc.scalar.activation(warm_out[:], zero[:], ACT.Silu)
        make_identity(nc, ident[:], nomemset=True)

        def entries(first, count):
            return offsets[:, first // 16 : (first + count) // 16]

        picked_rows = keep.tile([P, S], U8, name="picked_rows", align_bytes=64)
        nc.vector.tensor_copy(picked_rows[:], scale_table[:].indirect(offsets[:]))
        for q in range(4):
            src = SCALE_FIRST + 4 * q
            nc.sync.dma_start(x_scale[32 * q : 32 * q + 4, :].bitcast(I32), picked_rows[src : src + 4, :].bitcast(I32))

        w_bf = shared.tile([P, 4 * N], BF16, name="w_bf", align_bytes=64, offset=16 * N)
        w_codes = keep.tile([P, N], U32, name="w_codes", align_bytes=64)
        w_scale = keep.tile([P, N], U8, name="w_scale", align_bytes=64)

        per_stage = STAGE // BLOCK
        codes = {}

        def gather_words(first, count, pool, **place):
            piece = pool.tile([P, count], U32, name="codes%d" % first, align_bytes=64, **place)
            nc.vector.tensor_copy(piece[:], words[:].bitcast(U32).indirect(entries(first, count)))
            for k in range(first // BLOCK, (first + count) // BLOCK):
                codes[k] = piece[:, k * BLOCK - first : (k + 1) * BLOCK - first]
            return piece

        gather_words(STAGE, S - STAGE - BLOCK, keep)

        per_half = HALF // BLOCK
        turned = []
        for h in range(S // HALF):
            picked = keep.tile([P, HALF], F32, name="picked%d" % h)
            nc.scalar.activation(picked[:], stats[:].indirect(entries(h * HALF, HALF)), ACT.Copy)
            bank = psum.tile([P, per_half, P], F32, name="turned%d" % h, tag="turn%d" % h)
            for i in range(per_half):
                nc.tensor.transpose(bank[:, i, :], picked[:, i * BLOCK : (i + 1) * BLOCK], ident[:])
            turned.append(bank)

        gsum_row = psum.tile([P, N], F32, name="gsum_row", tag="gsum")
        nc.tensor.transpose(gsum_row[:], gsum_col[:, 0:1].to_broadcast([P, P]), ident[:])
        spread = psum.tile([P, 2, STAGE], F32, name="spread", tag="spread")
        neg_mean = shared.tile([P, STAGE], F32, name="neg_mean", offset=4 * STAGE)
        negs, prods, terms = [], {}, {}
        for h in range(S // HALF):
            first = h * per_half
            if h == 0:
                neg = keep.tile([P, per_half, 2], F32, name="neg0")
            else:
                neg = shared.tile([P, per_half, 2], F32, name="neg1", offset=0)
            negs.append(neg)
            nc.scalar.activation(neg[:], turned[h][:, :, MEAN_ROW : INV_ROW + 1], ACT.Copy, scale=-1.0)
            if h == 0:
                for c in range(2):
                    for i in range(per_stage):
                        nc.tensor.transpose(spread[:, c, i * BLOCK : (i + 1) * BLOCK], neg[:, i, c : c + 1].to_broadcast([P, P]), ident[:])
            if h == 0:
                nc.scalar.copy(w_bf[:].rearrange("p (c i j) -> p c j i", i=4, j=4), w_raw[:].rearrange("p (j c i) -> p c j i", i=4, j=4))
                nc.vector.quantize_mx(out=w_codes[:].bitcast(FP8X4), scales=w_scale[:], in_=w_bf[:])
                gather_words(S - BLOCK, BLOCK, shared, offset=16 * N)
                wide_codes = gather_words(0, STAGE, shared, offset=16 * N + 4 * BLOCK)
            for k in range(max(first, per_stage), first + per_half):
                prods[k] = shared.tile([P, 1], F32, name="prod%d" % k, offset=64 + 32 * k)
                nc.scalar.activation(prods[k][:], neg[:, k - first, 0:1], ACT.Copy, scale=neg[:, k - first, 1:2])
        for k in range(per_stage, BLOCKS):
            terms[k] = keep.tile([P, N], F32, name="term%d" % k)
            nc.scalar.activation(terms[k][:], gsum_row[:], ACT.Copy, scale=prods[k][:])
        nc.scalar.copy(neg_mean[:], spread[:, 0, :])

        ys = {}
        for s, tag in ((1, "a"), (2, "b"), (3, "turn0"), (0, "turn1")):
            ys[s] = psum.tile([P, STAGE], F32, name="y%d" % s, tag=tag)
            tokens = x_scale[:, s * STAGE : (s + 1) * STAGE]
            if s == 0:
                nc.tensor.matmul_mx(out=ys[s][:], lhsT=w_codes[:].bitcast(FP8X4), lhsT_scale=w_scale[:], rhs=wide_codes[:].bitcast(FP8X4), rhs_scale=tokens, start=True, stop=True)
            else:
                for i in range(per_stage):
                    cols = slice(i * BLOCK, (i + 1) * BLOCK)
                    nc.tensor.matmul_mx(out=ys[s][:, cols], lhsT=codes[s * per_stage + i].bitcast(FP8X4), lhsT_scale=tokens[:, cols], rhs=w_codes[:].bitcast(FP8X4), rhs_scale=w_scale[:], start=True, stop=True)

        def finish(values, first, count):
            res = keep.tile([P, count], F32, name="res%d" % first)
            nc.scalar.activation(res[:], values, ACT.Silu, bias=b_col[:], scale=-1.0)
            nc.sync.dma_start(out[:, first : first + count], res[:])

        centred = keep.tile([P, STAGE], F32, name="centred")
        scaled = keep.tile([P, STAGE], F32, name="scaled")
        for s, tag in ((1, "c"), (2, "d"), (3, "a")):
            fin = psum.tile([P, per_stage, BLOCK], F32, name="fin%d" % s, tag=tag)
            for i in range(per_stage):
                k = s * per_stage + i
                v = keep.tile([P, N], F32, name="v%d" % k)
                if k == BLOCKS - 1:
                    nc.vector.scalar_tensor_tensor(centred[:], neg_mean[:], gsum_col[:, 0:1], ys[0][:], ALU.mult, ALU.add)
                nc.vector.scalar_tensor_tensor(v[:], ys[s][:, i * BLOCK : (i + 1) * BLOCK], negs[k // per_half][:, k % per_half, 1:2], terms[k][:], ALU.mult, ALU.add)
                nc.tensor.transpose(fin[:, i, :], v[:], ident[:])
            finish(fin[:].rearrange("p i n -> p (i n)"), s * STAGE, STAGE)
        nc.vector.tensor_tensor(scaled[:], centred[:], spread[:, 1, :], ALU.mult)
        finish(scaled[:], 0, STAGE)
